import numpy as np
import ml_dtypes


def mxq(x, axis, fmt="e4m3"):
    dtype, down = {"e4m3": (ml_dtypes.float8_e4m3fn, 7), "e5m2": (ml_dtypes.float8_e5m2, 14)}[fmt]
    v = np.moveaxis(np.asarray(x, np.float32).astype(ml_dtypes.bfloat16).astype(np.float64), axis, -1)
    blocks = v.reshape(v.shape[:-1] + (-1, 32))
    amax = np.abs(blocks).max(-1, keepdims=True)
    byte = np.maximum(np.where(amax > 0, np.frexp(amax)[1] - 1 + 127, 0) - down, 1)
    scale = np.exp2(byte - 127.0)
    codes = (blocks / scale).astype(np.float32).astype(dtype).astype(np.float64)
    return np.moveaxis((codes * scale).reshape(v.shape), -1, axis)


WIDE = False


def mx_kscale(k):
    if not WIDE:
        return np.ones(k)
    levels = np.array([30, -30])
    if k % 512:
        return np.exp2(np.random.permutation(np.resize(levels, k // 32))).repeat(32)
    a = np.empty((k // 512, 16))
    for p in range(k // 512):
        a[p, :8] = np.random.permutation(np.resize(levels, 8))
        for g in range(8):
            far = levels[np.abs(levels - a[p, g]) >= 10]
            a[p, g + 8] = far[np.random.randint(len(far))]
    return np.exp2(a.ravel()).repeat(32)


BF16 = ml_dtypes.bfloat16


def bf(x):
    return np.asarray(x, np.float32).astype(BF16)


def f64(x):
    return np.asarray(x).astype(np.float64)


E2M1 = np.array([0.0, 0.5, 1.0, 1.5, 2.0, 3.0, 4.0, 6.0, -0.0, -0.5, -1.0, -1.5, -2.0, -3.0, -4.0, -6.0])


def pack_weight(w, fmt):
    k, n = w.shape
    w = f64(bf(w)).reshape(k // 32, 32, n)
    amax = np.abs(w).max(1)
    if fmt in ("e4m3", "e5m2"):
        byte = np.frexp(amax)[1] - 1 + 127 - (7 if fmt == "e4m3" else 14)
    else:
        mant, ex = np.frexp(amax / 6.0)
        byte = np.where(mant > 0.5, ex, ex - 1) + 127
    byte = np.clip(np.where(amax > 0, byte, 1), 1, 254)
    scaled = (w * np.exp2(127.0 - byte)[:, None, :]).reshape(k, n).astype(np.float32)
    by_word = np.ascontiguousarray(scaled.reshape(k // 512, 128, 4, n).transpose(0, 1, 3, 2))
    if fmt in ("e4m3", "e5m2"):
        words = by_word.astype(ml_dtypes.float8_e4m3fn if fmt == "e4m3" else ml_dtypes.float8_e5m2).view(np.uint8)
    else:
        c = by_word.astype(ml_dtypes.float4_e2m1fn).view(np.uint8) & 0xF
        words = c[..., 0::2] | (c[..., 1::2] << 4)
    return np.ascontiguousarray(words), np.ascontiguousarray(byte.astype(np.uint8).reshape(k // 512, 16, n))


def unpack_weight(words, scales, fmt):
    g, p, n, _ = words.shape
    if fmt in ("e4m3", "e5m2"):
        vals = np.ascontiguousarray(words).view(ml_dtypes.float8_e4m3fn if fmt == "e4m3" else ml_dtypes.float8_e5m2).astype(np.float64)
    else:
        nib = np.empty((g, p, n, 4), np.uint8)
        nib[..., 0::2] = words & 0xF
        nib[..., 1::2] = words >> 4
        vals = E2M1[nib]
    vals = vals * np.repeat(np.exp2(scales.astype(np.float64) - 127.0), 8, axis=1)[..., None]
    return vals.transpose(0, 1, 3, 2).reshape(g * 512, n)

def planes(Y):
    n, m = Y.shape
    b = f64(bf(Y)).reshape(n // 32, 32, m)
    amax = np.abs(b).max(1)
    byte = np.clip(np.where(amax > 0, np.frexp(amax)[1] - 1 + 127 - 7, 1), 1, 254)
    codes = (b * np.exp2(127.0 - byte)[:, None, :]).reshape(n, m).astype(np.float32).astype(ml_dtypes.float8_e4m3fn).view(np.uint8)
    words = codes.reshape(n // 512, 128, 4, m).transpose(0, 1, 3, 2)
    return np.ascontiguousarray(words), np.ascontiguousarray(byte.astype(np.uint8).reshape(n // 512, 16, m))


R, S, C = 2048, 1024, 1536


def setup_inputs():
    s = mx_kscale(R)
    G = np.random.randn(R, S) * np.exp(np.random.randn(R, S) - 1.0)
    g_words, g_scales = pack_weight(G / s[:, None], "e5m2")
    E = np.random.randn(R, C) / np.sqrt(R) * s[:, None]
    v = np.exp(0.8 * np.random.randn(C))
    D = np.random.randn(S, C) * np.sqrt(v)
    a = 0.3 + 0.4 * np.random.rand(S)
    return {"g_words": g_words, "g_scales": g_scales, "E": bf(E), "D": bf(D), "v": bf(v), "a": bf(a)}


def reference(g_words, g_scales, E, D, v, a):
    G = unpack_weight(g_words, g_scales, "e5m2")
    E, D, v, a = f64(E), f64(D), f64(v), f64(a)
    P = G.T @ mxq(E, 0, "e4m3")
    y = D - a[:, None] * (v[None, :] * P + D)
    words, scales = planes(y.T)
    return y, words, scales

@@ -1,0 +1,487 @@
+from contextlib import ExitStack
+
+import concourse.mybir as mybir
+from concourse.masks import make_identity
+
+R, S, C = 2048, 1024, 1536
+FLOPS = 2 * R * S * C
+
+F32 = mybir.dt.float32
+BF16 = mybir.dt.bfloat16
+I32 = mybir.dt.int32
+U32 = mybir.dt.uint32
+U8 = mybir.dt.uint8
+E4M3X4 = mybir.dt.float8_e4m3fn_x4
+E5M2X4 = mybir.dt.float8_e5m2_x4
+MULT = mybir.AluOpType.mult
+ADD = mybir.AluOpType.add
+
+P = 128
+PACK = 4
+W = 512
+PASSES = R // W
+GROUPS = C // W
+ROWS = S // P
+PAIRS = ROWS // 2
+TILES = GROUPS * ROWS
+
+
+def tile_ocean_tomography_prior_step_k2_kernel(tc, g_words, g_scales, E, D, v, a, out_0, out_1, out_2):
+    nc = tc.nc
+    with ExitStack() as ctx:
+        keep = ctx.enter_context(tc.tile_pool(name="keep", bufs=1))
+        work = ctx.enter_context(tc.tile_pool(name="work", bufs=3))
+        acc_pool = ctx.enter_context(tc.psum_pool(name="acc", bufs=6))
+        turn_pool = ctx.enter_context(tc.psum_pool(name="turn", bufs=2))
+        ctx.enter_context(tc.manual_schedule())
+
+        g_scale = keep.tile([P, PASSES, S], U8, align_bytes=64)
+        ident_f32 = keep.tile([P, P], F32)
+        ident_bf16 = keep.tile([P, P], BF16)
+        av_rows = keep.tile([P, P], BF16)
+        v_cols = keep.tile([P, C // P], BF16)
+        v_wide = keep.tile([P, C], BF16)
+        neg_a = keep.tile([P, ROWS], F32)
+        one_minus_a = keep.tile([P, ROWS], F32)
+
+        g_view = g_words.rearrange("k p n t -> p k (n t)").bitcast(I32)
+        d_view = D.rearrange("(m p) j -> p m j", p=P)
+        y_view = out_0.rearrange("(m p) j -> p m j", p=P)
+        words_view = out_1.rearrange("g p m t -> g p (m t)").bitcast(I32)
+        scales_view = out_2.bitcast(I32)
+
+        e_raw, e_mix, e_code, e_scale = {}, {}, {}, {}
+        g_code, d_sb, acc, step, y_sb, y_bf, turned, y_mix, y_code, y_scale, small = {}, {}, {}, {}, {}, {}, {}, {}, {}, {}, {}
+
+        def load_e(g, k):
+            e_raw[g, k] = keep.tile([P, PACK, W], BF16, name="e_raw_%d_%d" % (g, k))
+            nc.sync.dma_start(out=e_raw[g, k][:], in_=E[k * W:(k + 1) * W, g * W:(g + 1) * W].rearrange("(p t) j -> p t j", t=PACK))
+
+        def load_g(c):
+            g_code[c] = keep.tile([P, PASSES, 2 * P], U32, name="g_code_%d" % c, align_bytes=64)
+            nc.sync.dma_start(out=g_code[c][:].bitcast(I32), in_=g_view[:, :, c * 2 * P:(c + 1) * 2 * P])
+
+        def load_d(c, g0, g1):
+            d = keep.tile([P, 2, (g1 - g0) * W], BF16, name="d_%d_%d" % (c, g0))
+            nc.sync.dma_start(out=d[:], in_=d_view[:, 2 * c:2 * c + 2, g0 * W:g1 * W])
+            for g in range(g0, g1):
+                for h in range(2):
+                    d_sb[g * ROWS + 2 * c + h] = d[:, h, (g - g0) * W:(g - g0 + 1) * W]
+
+        def clear_scales():
+            nc.vector.memset(g_scale[:].bitcast(U32), 0)
+
+        def load_scales():
+            for q in range(4):
+                nc.sync.dma_start(out=g_scale[32 * q:32 * q + 4, :, :].bitcast(I32),
+                                  in_=g_scales[:, 4 * q:4 * q + 4, :].rearrange("k r n -> r k n").bitcast(I32))
+
+        def load_av():
+            nc.gpsimd.memset(av_rows[:], 0.0)
+            nc.gpsimd.dma_start(out=av_rows[0:ROWS, :], in_=a.rearrange("(m p) -> m p", p=P))
+            nc.gpsimd.dma_start(out=av_rows[ROWS:ROWS + C // P, :], in_=v.rearrange("(c p) -> c p", p=P))
+            make_identity(nc, ident_bf16[:])
+            make_identity(nc, ident_f32[:])
+
+        def turn_av():
+            small["av"] = acc_pool.tile([P, P], BF16, name="av_cols", tag="acc")
+            nc.tensor.transpose(small["av"][:], av_rows[:], ident_bf16[:])
+
+        def take_v():
+            nc.scalar.copy(out=v_cols[:], in_=small["av"][:, ROWS:ROWS + C // P])
+
+        def take_a():
+            nc.vector.tensor_scalar(out=neg_a[:], in0=small["av"][:, 0:ROWS], scalar1=-1.0, scalar2=None, op0=MULT)
+            nc.vector.tensor_scalar(out=one_minus_a[:], in0=small["av"][:, 0:ROWS], scalar1=-1.0, scalar2=1.0, op0=MULT, op1=ADD)
+
+        def spread_v(g0, g1):
+            small["v", g0] = turn_pool.tile([P, (g1 - g0) * W], BF16, name="v_psum", tag="turn")
+            for c in range(g0 * PACK, g1 * PACK):
+                cc = c - g0 * PACK
+                nc.tensor.transpose(small["v", g0][:, cc * P:(cc + 1) * P], v_cols[:, c:c + 1].to_broadcast([P, P]), ident_bf16[:])
+
+        def keep_v(g0, g1):
+            nc.scalar.copy(out=v_wide[:, g0 * W:g1 * W], in_=small["v", g0][:])
+
+        def interleave(g, k, c0, c1, eng):
+            if (g, k) not in e_mix:
+                e_mix[g, k] = work.tile([P, W, PACK], BF16, name="e_mix", tag="e_mix", bufs=4, align_bytes=64)
+            dst = e_mix[g, k][:, c0:c1, :].rearrange("p (c i) t -> p c t i", i=4)
+            src = e_raw[g, k][:, :, c0:c1].rearrange("p t (c i) -> p c t i", i=4)
+            if eng == "v":
+                nc.vector.tensor_copy(out=dst, in_=src)
+            else:
+                nc.scalar.copy(out=dst, in_=src)
+
+        def quantize_e(g, k):
+            e_code[g, k] = keep.tile([P, W], U32, name="e_code_%d_%d" % (g, k), align_bytes=64)
+            e_scale[g, k] = keep.tile([P, W], U8, name="e_scale_%d_%d" % (g, k), align_bytes=64)
+            nc.vector.quantize_mx(out=e_code[g, k][:].bitcast(E4M3X4), scales=e_scale[g, k][:],
+                                  in_=e_mix[g, k][:].rearrange("p c t -> p (c t)"))
+
+        def matmul(n, k):
+            g, m = divmod(n, ROWS)
+            if k == 0:
+                acc[n] = acc_pool.tile([P, W], F32, name="acc", tag="acc")
+            c, h = divmod(m, 2)
+            nc.tensor.matmul_mx(out=acc[n][:], lhsT=g_code[c][:, k, h * P:(h + 1) * P].bitcast(E5M2X4),
+                                lhsT_scale=g_scale[:, k, m * P:(m + 1) * P],
+                                rhs=e_code[g, k][:].bitcast(E4M3X4), rhs_scale=e_scale[g, k][:],
+                                start=(k == 0), stop=(k == PASSES - 1))
+
+        def scale_product(n):
+            g, m = divmod(n, ROWS)
+            step[n] = work.tile([P, W], F32, name="step", tag="step", bufs=3)
+            nc.vector.scalar_tensor_tensor(out=step[n][:], in0=acc[n][:], scalar=neg_a[:, m:m + 1],
+                                           in1=v_wide[:, g * W:(g + 1) * W], op0=MULT, op1=MULT)
+
+        def add_prior(n):
+            g, m = divmod(n, ROWS)
+            if m % 2 == 0:
+                y_sb[n // 2] = keep.tile([P, 2, W], F32, name="y_%d" % (n // 2))
+            nc.vector.scalar_tensor_tensor(out=y_sb[n // 2][:, m % 2, :], in0=d_sb[n], scalar=one_minus_a[:, m:m + 1],
+                                           in1=step[n][:], op0=MULT, op1=ADD)
+
+        def round_y(n, eng):
+            y_bf[n] = work.tile([P, W], BF16, name="y_bf", tag="y_bf", bufs=6)
+            dst = y_bf[n][:].rearrange("p (u c e) -> p u c e", u=2, e=2)
+            src = y_sb[n // 2][:, n % 2, :].rearrange("p (c u e) -> p u c e", u=2, e=2)
+            if eng == "v":
+                nc.vector.tensor_copy(out=dst, in_=src)
+            else:
+                nc.scalar.copy(out=dst, in_=src)
+
+        def turn_y(q):
+            turned[q] = turn_pool.tile([P, 2, 2, P], F32, name="turned", tag="turn")
+            for h in range(2):
+                words = y_bf[2 * q + h][:].bitcast(F32)
+                for u in range(2):
+                    nc.tensor.transpose(turned[q][:, h, u, :], words[:, u * P:(u + 1) * P], ident_f32[:])
+
+        def gather_y(q):
+            y_mix[q] = work.tile([P, 2 * W], BF16, name="y_mix", tag="y_mix", bufs=3, align_bytes=64)
+            nc.scalar.copy(out=y_mix[q][:].bitcast(F32).rearrange("p (h i u) -> p h i u", h=2, u=2),
+                           in_=turned[q][:].rearrange("p h u i -> p h i u"))
+
+        def quantize_y(q):
+            g, c = divmod(q, PAIRS)
+            if c == 0:
+                y_code[g] = keep.tile([P, S], U32, name="y_code_%d" % g, align_bytes=64)
+                y_scale[g] = keep.tile([P, 2 * P], U8, name="y_scale_%d" % g, align_bytes=64)
+            nc.vector.quantize_mx(out=y_code[g][:, c * 2 * P:(c + 1) * 2 * P].bitcast(E4M3X4),
+                                  scales=y_scale[g][4 * c:P, :], in_=y_mix[q][:])
+
+        def store_y(q):
+            g, c = divmod(q, PAIRS)
+            nc.sync.dma_start(out=y_view[:, 2 * c:2 * c + 2, g * W:(g + 1) * W], in_=y_sb[q][:])
+
+        def store_words(g, c0, c1):
+            nc.sync.dma_start(out=words_view[g, :, c0 * 2 * P:c1 * 2 * P], in_=y_code[g][:, c0 * 2 * P:c1 * 2 * P].bitcast(I32))
+
+        def store_scales(g, q):
+            nc.sync.dma_start(out=scales_view[g, 4 * q:4 * q + 4, :].rearrange("r (c m) -> c r m", c=PAIRS),
+                              in_=y_scale[g][32 * q:32 * q + 16, :].bitcast(I32))
+
+        clear_scales()
+        load_av()
+        load_e(0, 0)
+        load_e(0, 3)
+        load_e(0, 1)
+        load_e(0, 2)
+        load_scales()
+        load_g(0)
+        load_e(1, 0)
+        load_g(1)
+        load_e(1, 1)
+        interleave(0, 0, 0, 256, "v")
+        interleave(0, 0, 256, 512, "v")
+        turn_av()
+        load_d(0, 0, 1)
+        interleave(0, 3, 0, 256, "s")
+        take_a()
+        quantize_e(0, 0)
+        load_g(2)
+        interleave(0, 1, 0, 256, "v")
+        take_v()
+        interleave(0, 3, 256, 512, "s")
+        spread_v(0, 1)
+        interleave(0, 1, 256, 512, "v")
+        spread_v(1, 3)
+        load_d(1, 0, 1)
+        interleave(0, 2, 0, 256, "v")
+        keep_v(0, 1)
+        load_e(1, 2)
+        interleave(0, 2, 256, 512, "v")
+        keep_v(1, 3)
+        quantize_e(0, 1)
+        load_e(1, 3)
+        matmul(0, 0)
+        quantize_e(0, 2)
+        matmul(1, 0)
+        matmul(0, 1)
+        quantize_e(0, 3)
+        matmul(1, 1)
+        load_g(3)
+        matmul(0, 2)
+        interleave(1, 0, 0, 256, "s")
+        interleave(1, 0, 256, 512, "v")
+        matmul(1, 2)
+        matmul(0, 3)
+        matmul(1, 3)
+        load_d(3, 0, 1)
+        scale_product(0)
+        matmul(2, 0)
+        matmul(2, 1)
+        quantize_e(1, 0)
+        matmul(2, 2)
+        matmul(2, 3)
+        load_d(2, 0, 1)
+        scale_product(1)
+        matmul(3, 0)
+        interleave(1, 1, 0, 256, "s")
+        matmul(3, 1)
+        load_e(2, 0)
+        matmul(3, 2)
+        add_prior(0)
+        matmul(3, 3)
+        scale_product(2)
+        interleave(1, 1, 256, 512, "s")
+        load_e(2, 1)
+        add_prior(1)
+        matmul(4, 0)
+        matmul(4, 1)
+        load_e(2, 2)
+        scale_product(3)
+        matmul(4, 2)
+        round_y(0, "s")
+        matmul(4, 3)
+        quantize_e(1, 1)
+        matmul(5, 0)
+        round_y(1, "s")
+        matmul(5, 1)
+        load_d(3, 1, 3)
+        add_prior(2)
+        matmul(5, 2)
+        interleave(1, 2, 0, 256, "s")
+        turn_y(0)
+        scale_product(4)
+        matmul(5, 3)
+        load_d(0, 1, 3)
+        interleave(1, 3, 256, 512, "v")
+        interleave(1, 2, 256, 512, "s")
+        add_prior(3)
+        load_e(2, 3)
+        matmul(6, 0)
+        scale_product(5)
+        interleave(1, 3, 0, 256, "s")
+        matmul(6, 1)
+        load_d(2, 1, 3)
+        matmul(6, 2)
+        quantize_e(1, 2)
+        matmul(6, 3)
+        load_d(1, 1, 3)
+        matmul(7, 0)
+        add_prior(4)
+        gather_y(0)
+        matmul(7, 1)
+        matmul(7, 2)
+        quantize_e(1, 3)
+        round_y(2, "s")
+        matmul(7, 3)
+        store_y(0)
+        matmul(8, 0)
+        quantize_y(0)
+        interleave(2, 0, 0, 256, "s")
+        matmul(8, 1)
+        scale_product(6)
+        matmul(8, 2)
+        matmul(8, 3)
+        add_prior(5)
+        store_y(1)
+        matmul(9, 0)
+        interleave(2, 0, 256, 512, "s")
+        matmul(9, 1)
+        scale_product(7)
+        matmul(9, 2)
+        matmul(9, 3)
+        add_prior(6)
+        matmul(10, 0)
+        store_y(2)
+        interleave(2, 1, 0, 256, "s")
+        matmul(10, 1)
+        quantize_e(2, 0)
+        matmul(10, 2)
+        matmul(10, 3)
+        scale_product(8)
+        matmul(11, 0)
+        interleave(2, 1, 256, 512, "s")
+        matmul(11, 1)
+        add_prior(7)
+        matmul(11, 2)
+        matmul(11, 3)
+        scale_product(9)
+        store_y(3)
+        matmul(12, 0)
+        matmul(12, 1)
+        interleave(2, 2, 0, 256, "s")
+        add_prior(8)
+        matmul(12, 2)
+        matmul(12, 3)
+        quantize_e(2, 1)
+        matmul(13, 0)
+        matmul(13, 1)
+        interleave(2, 2, 256, 512, "s")
+        scale_product(10)
+        matmul(13, 2)
+        matmul(13, 3)
+        add_prior(9)
+        matmul(14, 0)
+        matmul(14, 1)
+        scale_product(11)
+        interleave(2, 3, 0, 256, "s")
+        store_y(4)
+        matmul(14, 2)
+        matmul(14, 3)
+        quantize_e(2, 2)
+        matmul(15, 0)
+        matmul(15, 1)
+        add_prior(10)
+        interleave(2, 3, 256, 512, "s")
+        matmul(15, 2)
+        matmul(15, 3)
+        scale_product(12)
+        matmul(16, 0)
+        matmul(16, 1)
+        add_prior(11)
+        round_y(3, "s")
+        matmul(16, 2)
+        quantize_e(2, 3)
+        round_y(4, "s")
+        store_y(5)
+        turn_y(1)
+        scale_product(13)
+        round_y(5, "s")
+        matmul(16, 3)
+        matmul(17, 0)
+        add_prior(12)
+        gather_y(1)
+        turn_y(2)
+        scale_product(14)
+        round_y(6, "s")
+        matmul(17, 1)
+        matmul(17, 2)
+        quantize_y(1)
+        gather_y(2)
+        matmul(17, 3)
+        add_prior(13)
+        matmul(18, 0)
+        round_y(7, "s")
+        matmul(18, 1)
+        quantize_y(2)
+        store_y(6)
+        matmul(18, 2)
+        scale_product(15)
+        round_y(8, "s")
+        turn_y(3)
+        add_prior(14)
+        round_y(9, "s")
+        matmul(18, 3)
+        matmul(19, 0)
+        scale_product(16)
+        gather_y(3)
+        turn_y(4)
+        add_prior(15)
+        round_y(10, "s")
+        matmul(19, 1)
+        quantize_y(3)
+        matmul(19, 2)
+        gather_y(4)
+        store_y(7)
+        matmul(19, 3)
+        scale_product(17)
+        store_words(0, 0, 4)
+        store_scales(0, 0)
+        matmul(20, 0)
+        round_y(11, "s")
+        store_scales(0, 1)
+        store_scales(0, 2)
+        matmul(20, 1)
+        quantize_y(4)
+        store_scales(0, 3)
+        matmul(20, 2)
+        add_prior(16)
+        round_y(12, "s")
+        turn_y(5)
+        scale_product(18)
+        round_y(13, "s")
+        matmul(20, 3)
+        matmul(21, 0)
+        add_prior(17)
+        gather_y(5)
+        turn_y(6)
+        scale_product(19)
+        round_y(14, "s")
+        store_y(8)
+        matmul(21, 1)
+        quantize_y(5)
+        matmul(21, 2)
+        gather_y(6)
+        matmul(21, 3)
+        add_prior(18)
+        matmul(22, 0)
+        round_y(15, "s")
+        quantize_y(6)
+        matmul(22, 1)
+        matmul(22, 2)
+        scale_product(20)
+        round_y(16, "s")
+        turn_y(7)
+        add_prior(19)
+        round_y(17, "s")
+        matmul(22, 3)
+        scale_product(21)
+        matmul(23, 0)
+        gather_y(7)
+        store_y(9)
+        turn_y(8)
+        add_prior(20)
+        round_y(18, "s")
+        matmul(23, 1)
+        quantize_y(7)
+        matmul(23, 2)
+        gather_y(8)
+        scale_product(22)
+        matmul(23, 3)
+        store_words(1, 0, 4)
+        store_scales(1, 0)
+        round_y(19, "s")
+        store_scales(1, 1)
+        store_scales(1, 2)
+        quantize_y(8)
+        store_scales(1, 3)
+        add_prior(21)
+        round_y(20, "s")
+        turn_y(9)
+        scale_product(23)
+        round_y(21, "s")
+        store_y(10)
+        add_prior(22)
+        gather_y(9)
+        turn_y(10)
+        add_prior(23)
+        round_y(22, "v")
+        gather_y(10)
+        store_y(11)
+        round_y(23, "v")
+        quantize_y(9)
+        turn_y(11)
+        quantize_y(10)
+        store_words(2, 0, 2)
+        store_words(2, 2, 3)
+        gather_y(11)
+        quantize_y(11)
+        store_words(2, 3, 4)
+        store_scales(2, 0)
+        store_scales(2, 1)
+        store_scales(2, 2)
+        store_scales(2, 3)

@@ -50,16 +50,19 @@ def tile_ocean_tomography_prior_step_k2_kernel(tc, g_words, g_scales, E, D, v, a
         words_view = out_1.rearrange("g p m t -> g p (m t)").bitcast(I32)
         scales_view = out_2.bitcast(I32)
 
-        e_raw, e_mix, e_code, e_scale = {}, {}, {}, {}
+        e_raw, e_mix, e_code, e_scale, y_tile = {}, {}, {}, {}, {}
         g_code, d_sb, acc, step, y_sb, y_bf, turned, y_mix, y_code, y_scale, small = {}, {}, {}, {}, {}, {}, {}, {}, {}, {}, {}
 
         def load_e(g, k):
             e_raw[g, k] = keep.tile([P, PACK, W], BF16, name="e_raw_%d_%d" % (g, k))
             nc.sync.dma_start(out=e_raw[g, k][:], in_=E[k * W:(k + 1) * W, g * W:(g + 1) * W].rearrange("(p t) j -> p t j", t=PACK))
 
-        def load_g(c):
-            g_code[c] = keep.tile([P, PASSES, 2 * P], U32, name="g_code_%d" % c, align_bytes=64)
-            nc.sync.dma_start(out=g_code[c][:].bitcast(I32), in_=g_view[:, :, c * 2 * P:(c + 1) * 2 * P])
+        def load_g(m0, m1):
+            codes = keep.tile([P, PASSES, (m1 - m0) * P], U32, name="g_code_%d" % m0, align_bytes=64)
+            nc.sync.dma_start(out=codes[:].bitcast(I32), in_=g_view[:, :, m0 * P:m1 * P])
+            for m in range(m0, m1):
+                for k in range(PASSES):
+                    g_code[m, k] = codes[:, k, (m - m0) * P:(m - m0 + 1) * P]
 
         def load_d(c, g0, g1):
             d = keep.tile([P, 2, (g1 - g0) * W], BF16, name="d_%d_%d" % (c, g0))
@@ -68,20 +71,24 @@ def tile_ocean_tomography_prior_step_k2_kernel(tc, g_words, g_scales, E, D, v, a
                 for h in range(2):
                     d_sb[g * ROWS + 2 * c + h] = d[:, h, (g - g0) * W:(g - g0 + 1) * W]
 
-        def clear_scales():
+        def clear():
+            nc.vector.memset(ident_f32[:], 0.0)
             nc.vector.memset(g_scale[:].bitcast(U32), 0)
 
-        def load_scales():
-            for q in range(4):
-                nc.sync.dma_start(out=g_scale[32 * q:32 * q + 4, :, :].bitcast(I32),
-                                  in_=g_scales[:, 4 * q:4 * q + 4, :].rearrange("k r n -> r k n").bitcast(I32))
+        def load_scales(q, m0, m1):
+            nc.sync.dma_start(out=g_scale[32 * q:32 * q + 4, :, m0 * P:m1 * P].bitcast(I32),
+                              in_=g_scales[:, 4 * q:4 * q + 4, m0 * P:m1 * P].rearrange("k r n -> r k n").bitcast(I32))
+
+        def prepare():
+            nc.gpsimd.memset(av_rows[:], 0.0)
+            make_identity(nc, ident_f32[:], nomemset=True)
+            nc.vector.tensor_copy(out=ident_bf16[:], in_=ident_f32[:])
 
         def load_av():
-            nc.gpsimd.memset(av_rows[:], 0.0)
-            nc.gpsimd.dma_start(out=av_rows[0:ROWS, :], in_=a.rearrange("(m p) -> m p", p=P))
-            nc.gpsimd.dma_start(out=av_rows[ROWS:ROWS + C // P, :], in_=v.rearrange("(c p) -> c p", p=P))
-            make_identity(nc, ident_bf16[:])
-            make_identity(nc, ident_f32[:])
+            v_rows = v.rearrange("(c p) -> c p", p=P)
+            nc.sync.dma_start(out=av_rows[0:ROWS, :], in_=a.rearrange("(m p) -> m p", p=P))
+            nc.sync.dma_start(out=av_rows[ROWS:2 * ROWS, :], in_=v_rows[0:ROWS, :])
+            nc.sync.dma_start(out=av_rows[2 * ROWS:ROWS + C // P, :], in_=v_rows[ROWS:C // P, :])
 
         def turn_av():
             small["av"] = acc_pool.tile([P, P], BF16, name="av_cols", tag="acc")
@@ -123,8 +130,7 @@ def tile_ocean_tomography_prior_step_k2_kernel(tc, g_words, g_scales, E, D, v, a
             g, m = divmod(n, ROWS)
             if k == 0:
                 acc[n] = acc_pool.tile([P, W], F32, name="acc", tag="acc")
-            c, h = divmod(m, 2)
-            nc.tensor.matmul_mx(out=acc[n][:], lhsT=g_code[c][:, k, h * P:(h + 1) * P].bitcast(E5M2X4),
+            nc.tensor.matmul_mx(out=acc[n][:], lhsT=g_code[m, k].bitcast(E5M2X4),
                                 lhsT_scale=g_scale[:, k, m * P:(m + 1) * P],
                                 rhs=e_code[g, k][:].bitcast(E4M3X4), rhs_scale=e_scale[g, k][:],
                                 start=(k == 0), stop=(k == PASSES - 1))
@@ -137,350 +143,359 @@ def tile_ocean_tomography_prior_step_k2_kernel(tc, g_words, g_scales, E, D, v, a
 
         def add_prior(n):
             g, m = divmod(n, ROWS)
-            if m % 2 == 0:
-                y_sb[n // 2] = keep.tile([P, 2, W], F32, name="y_%d" % (n // 2))
-            nc.vector.scalar_tensor_tensor(out=y_sb[n // 2][:, m % 2, :], in0=d_sb[n], scalar=one_minus_a[:, m:m + 1],
+            key = (m // 2, g // 2)
+            if key not in y_sb:
+                y_sb[key] = keep.tile([P, 2, (2 - g // 2) * W], F32, name="y_%d_%d" % key)
+            y_tile[n] = y_sb[key][:, m % 2, (g % 2) * W:(g % 2 + 1) * W]
+            nc.vector.scalar_tensor_tensor(out=y_tile[n], in0=d_sb[n], scalar=one_minus_a[:, m:m + 1],
                                            in1=step[n][:], op0=MULT, op1=ADD)
 
         def round_y(n, eng):
             y_bf[n] = work.tile([P, W], BF16, name="y_bf", tag="y_bf", bufs=6)
             dst = y_bf[n][:].rearrange("p (u c e) -> p u c e", u=2, e=2)
-            src = y_sb[n // 2][:, n % 2, :].rearrange("p (c u e) -> p u c e", u=2, e=2)
+            src = y_tile[n].rearrange("p (c u e) -> p u c e", u=2, e=2)
             if eng == "v":
                 nc.vector.tensor_copy(out=dst, in_=src)
+            elif eng == "g":
+                nc.gpsimd.tensor_scalar(out=dst, in0=src, scalar1=1.0, scalar2=0.0, op0=MULT, op1=ADD)
             else:
                 nc.scalar.copy(out=dst, in_=src)
 
-        def turn_y(q):
-            turned[q] = turn_pool.tile([P, 2, 2, P], F32, name="turned", tag="turn")
-            for h in range(2):
-                words = y_bf[2 * q + h][:].bitcast(F32)
+        def turn_y(n, count):
+            turned[n] = turn_pool.tile([P, count, 2, P], F32, name="turned", tag="turn")
+            for h in range(count):
+                words = y_bf[n + h][:].bitcast(F32)
                 for u in range(2):
-                    nc.tensor.transpose(turned[q][:, h, u, :], words[:, u * P:(u + 1) * P], ident_f32[:])
+                    nc.tensor.transpose(turned[n][:, h, u, :], words[:, u * P:(u + 1) * P], ident_f32[:])
 
-        def gather_y(q):
-            y_mix[q] = work.tile([P, 2 * W], BF16, name="y_mix", tag="y_mix", bufs=3, align_bytes=64)
-            nc.scalar.copy(out=y_mix[q][:].bitcast(F32).rearrange("p (h i u) -> p h i u", h=2, u=2),
-                           in_=turned[q][:].rearrange("p h u i -> p h i u"))
+        def gather_y(n, count):
+            y_mix[n] = work.tile([P, count * W], BF16, name="y_mix", tag="y_mix", bufs=3, align_bytes=64)
+            nc.scalar.copy(out=y_mix[n][:].bitcast(F32).rearrange("p (h i u) -> p h i u", h=count, u=2),
+                           in_=turned[n][:].rearrange("p h u i -> p h i u"))
 
-        def quantize_y(q):
-            g, c = divmod(q, PAIRS)
-            if c == 0:
+        def quantize_y(n, count):
+            g, m = divmod(n, ROWS)
+            if m == 0:
                 y_code[g] = keep.tile([P, S], U32, name="y_code_%d" % g, align_bytes=64)
                 y_scale[g] = keep.tile([P, 2 * P], U8, name="y_scale_%d" % g, align_bytes=64)
-            nc.vector.quantize_mx(out=y_code[g][:, c * 2 * P:(c + 1) * 2 * P].bitcast(E4M3X4),
-                                  scales=y_scale[g][4 * c:P, :], in_=y_mix[q][:])
+            nc.vector.quantize_mx(out=y_code[g][:, m * P:(m + count) * P].bitcast(E4M3X4),
+                                  scales=y_scale[g][4 * (m // 2):P, (m % 2) * P:(m % 2 + count) * P], in_=y_mix[n][:])
 
-        def store_y(q):
-            g, c = divmod(q, PAIRS)
-            nc.sync.dma_start(out=y_view[:, 2 * c:2 * c + 2, g * W:(g + 1) * W], in_=y_sb[q][:])
+        def store_y(m0, m1, g0, g1):
+            nc.sync.dma_start(out=y_view[:, m0:m1, g0 * W:g1 * W], in_=y_sb[m0 // 2, g0 // 2][:, m0 % 2:m0 % 2 + m1 - m0, (g0 % 2) * W:(g0 % 2 + g1 - g0) * W])
 
-        def store_words(g, c0, c1):
-            nc.sync.dma_start(out=words_view[g, :, c0 * 2 * P:c1 * 2 * P], in_=y_code[g][:, c0 * 2 * P:c1 * 2 * P].bitcast(I32))
+        def store_words(g, m0, m1):
+            nc.sync.dma_start(out=words_view[g, :, m0 * P:m1 * P], in_=y_code[g][:, m0 * P:m1 * P].bitcast(I32))
 
         def store_scales(g, q):
             nc.sync.dma_start(out=scales_view[g, 4 * q:4 * q + 4, :].rearrange("r (c m) -> c r m", c=PAIRS),
-                              in_=y_scale[g][32 * q:32 * q + 16, :].bitcast(I32))
+                          in_=y_scale[g][32 * q:32 * q + 16, :].bitcast(I32))
 
-        clear_scales()
-        load_av()
+        clear()
+        prepare()
         load_e(0, 0)
-        load_e(0, 3)
+        load_av()
+        turn_av()
         load_e(0, 1)
         load_e(0, 2)
-        load_scales()
-        load_g(0)
-        load_e(1, 0)
-        load_g(1)
-        load_e(1, 1)
-        interleave(0, 0, 0, 256, "v")
+        load_g(0, 2)
+        load_scales(0, 0, 8)
+        load_scales(1, 0, 8)
+        load_scales(2, 0, 8)
+        load_scales(3, 0, 8)
+        load_e(0, 3)
         interleave(0, 0, 256, 512, "v")
-        turn_av()
-        load_d(0, 0, 1)
-        interleave(0, 3, 0, 256, "s")
-        take_a()
-        quantize_e(0, 0)
-        load_g(2)
-        interleave(0, 1, 0, 256, "v")
+        interleave(0, 0, 0, 256, "s")
         take_v()
-        interleave(0, 3, 256, 512, "s")
         spread_v(0, 1)
-        interleave(0, 1, 256, 512, "v")
         spread_v(1, 3)
-        load_d(1, 0, 1)
-        interleave(0, 2, 0, 256, "v")
+        load_g(2, 4)
+        interleave(0, 1, 0, 256, "v")
+        interleave(0, 1, 256, 512, "v")
+        load_e(1, 0)
+        interleave(0, 2, 0, 256, "s")
         keep_v(0, 1)
-        load_e(1, 2)
         interleave(0, 2, 256, 512, "v")
-        keep_v(1, 3)
+        quantize_e(0, 0)
         quantize_e(0, 1)
-        load_e(1, 3)
-        matmul(0, 0)
+        take_a()
+        load_d(0, 0, 1)
+        load_g(4, 6)
         quantize_e(0, 2)
+        load_d(1, 0, 1)
+        load_g(6, 8)
+        load_d(2, 0, 1)
+        matmul(0, 0)
         matmul(1, 0)
         matmul(0, 1)
-        quantize_e(0, 3)
+        load_e(1, 1)
+        interleave(0, 3, 0, 192, "s")
+        keep_v(1, 3)
+        interleave(0, 3, 192, 512, "v")
         matmul(1, 1)
-        load_g(3)
         matmul(0, 2)
-        interleave(1, 0, 0, 256, "s")
-        interleave(1, 0, 256, 512, "v")
         matmul(1, 2)
+        quantize_e(0, 3)
+        load_e(1, 3)
         matmul(0, 3)
         matmul(1, 3)
-        load_d(3, 0, 1)
-        scale_product(0)
         matmul(2, 0)
+        scale_product(0)
+        load_e(1, 2)
         matmul(2, 1)
-        quantize_e(1, 0)
+        interleave(1, 0, 0, 256, "s")
         matmul(2, 2)
-        matmul(2, 3)
-        load_d(2, 0, 1)
         scale_product(1)
-        matmul(3, 0)
-        interleave(1, 1, 0, 256, "s")
-        matmul(3, 1)
         load_e(2, 0)
-        matmul(3, 2)
+        matmul(2, 3)
+        matmul(3, 0)
         add_prior(0)
-        matmul(3, 3)
+        matmul(3, 1)
+        interleave(1, 0, 256, 512, "s")
+        matmul(3, 2)
         scale_product(2)
-        interleave(1, 1, 256, 512, "s")
-        load_e(2, 1)
+        matmul(3, 3)
+        load_d(3, 0, 1)
         add_prior(1)
         matmul(4, 0)
-        matmul(4, 1)
-        load_e(2, 2)
-        scale_product(3)
-        matmul(4, 2)
         round_y(0, "s")
-        matmul(4, 3)
-        quantize_e(1, 1)
-        matmul(5, 0)
-        round_y(1, "s")
-        matmul(5, 1)
-        load_d(3, 1, 3)
-        add_prior(2)
-        matmul(5, 2)
-        interleave(1, 2, 0, 256, "s")
-        turn_y(0)
-        scale_product(4)
-        matmul(5, 3)
+        matmul(4, 1)
+        quantize_e(1, 0)
         load_d(0, 1, 3)
-        interleave(1, 3, 256, 512, "v")
-        interleave(1, 2, 256, 512, "s")
-        add_prior(3)
-        load_e(2, 3)
-        matmul(6, 0)
-        scale_product(5)
-        interleave(1, 3, 0, 256, "s")
-        matmul(6, 1)
-        load_d(2, 1, 3)
-        matmul(6, 2)
-        quantize_e(1, 2)
-        matmul(6, 3)
+        matmul(4, 2)
+        round_y(1, "s")
+        matmul(4, 3)
+        scale_product(3)
+        matmul(5, 0)
+        turn_y(0, 2)
+        add_prior(2)
+        load_e(2, 1)
+        matmul(5, 1)
+        scale_product(4)
+        matmul(5, 2)
+        gather_y(0, 2)
+        matmul(5, 3)
         load_d(1, 1, 3)
+        add_prior(3)
+        matmul(6, 0)
+        round_y(2, "s")
+        matmul(6, 1)
+        scale_product(5)
+        matmul(6, 2)
+        round_y(3, "s")
+        matmul(6, 3)
         matmul(7, 0)
+        load_e(2, 2)
+        interleave(1, 1, 0, 256, "s")
+        interleave(1, 1, 256, 512, "v")
+        turn_y(2, 2)
         add_prior(4)
-        gather_y(0)
         matmul(7, 1)
         matmul(7, 2)
-        quantize_e(1, 3)
-        round_y(2, "s")
-        matmul(7, 3)
-        store_y(0)
-        matmul(8, 0)
-        quantize_y(0)
-        interleave(2, 0, 0, 256, "s")
-        matmul(8, 1)
+        gather_y(2, 2)
         scale_product(6)
-        matmul(8, 2)
-        matmul(8, 3)
+        matmul(7, 3)
+        load_e(2, 3)
+        matmul(8, 0)
+        round_y(4, "s")
+        quantize_e(1, 1)
         add_prior(5)
-        store_y(1)
-        matmul(9, 0)
-        interleave(2, 0, 256, 512, "s")
-        matmul(9, 1)
+        load_d(3, 1, 3)
+        matmul(8, 1)
+        interleave(1, 2, 0, 256, "s")
+        interleave(1, 2, 256, 512, "v")
+        interleave(1, 3, 256, 512, "v")
+        interleave(1, 3, 0, 256, "s")
+        load_d(2, 1, 3)
+        quantize_e(1, 2)
         scale_product(7)
-        matmul(9, 2)
-        matmul(9, 3)
+        store_y(4, 6, 0, 1)
+        matmul(8, 2)
+        interleave(2, 0, 0, 256, "s")
+        quantize_e(1, 3)
         add_prior(6)
-        matmul(10, 0)
-        store_y(2)
-        interleave(2, 1, 0, 256, "s")
-        matmul(10, 1)
-        quantize_e(2, 0)
-        matmul(10, 2)
-        matmul(10, 3)
+        matmul(8, 3)
+        interleave(2, 0, 256, 512, "s")
+        quantize_y(0, 2)
+        quantize_y(2, 2)
+        matmul(9, 0)
         scale_product(8)
-        matmul(11, 0)
-        interleave(2, 1, 256, 512, "s")
-        matmul(11, 1)
+        matmul(9, 1)
+        interleave(2, 1, 0, 256, "s")
+        matmul(9, 2)
+        quantize_e(2, 0)
+        matmul(9, 3)
+        matmul(10, 0)
         add_prior(7)
-        matmul(11, 2)
-        matmul(11, 3)
+        matmul(10, 1)
+        interleave(2, 1, 256, 512, "s")
+        matmul(10, 2)
         scale_product(9)
-        store_y(3)
-        matmul(12, 0)
-        matmul(12, 1)
-        interleave(2, 2, 0, 256, "s")
+        store_y(6, 8, 0, 1)
+        matmul(10, 3)
+        matmul(11, 0)
         add_prior(8)
-        matmul(12, 2)
-        matmul(12, 3)
+        matmul(11, 1)
+        matmul(11, 2)
+        round_y(5, "s")
         quantize_e(2, 1)
-        matmul(13, 0)
-        matmul(13, 1)
-        interleave(2, 2, 256, 512, "s")
+        matmul(11, 3)
+        matmul(12, 0)
+        interleave(2, 2, 0, 256, "s")
         scale_product(10)
-        matmul(13, 2)
-        matmul(13, 3)
+        turn_y(4, 2)
         add_prior(9)
+        matmul(12, 1)
+        matmul(12, 2)
+        interleave(2, 2, 256, 512, "s")
+        scale_product(11)
+        matmul(12, 3)
+        store_y(0, 2, 0, 2)
+        matmul(13, 0)
+        add_prior(10)
+        matmul(13, 1)
+        matmul(13, 2)
+        interleave(2, 3, 0, 256, "s")
+        quantize_e(2, 2)
+        matmul(13, 3)
         matmul(14, 0)
         matmul(14, 1)
-        scale_product(11)
-        interleave(2, 3, 0, 256, "s")
-        store_y(4)
+        scale_product(12)
         matmul(14, 2)
+        interleave(2, 3, 256, 512, "s")
         matmul(14, 3)
-        quantize_e(2, 2)
+        add_prior(11)
         matmul(15, 0)
         matmul(15, 1)
-        add_prior(10)
-        interleave(2, 3, 256, 512, "s")
-        matmul(15, 2)
-        matmul(15, 3)
-        scale_product(12)
-        matmul(16, 0)
-        matmul(16, 1)
-        add_prior(11)
-        round_y(3, "s")
-        matmul(16, 2)
-        quantize_e(2, 3)
-        round_y(4, "s")
-        store_y(5)
-        turn_y(1)
         scale_product(13)
-        round_y(5, "s")
-        matmul(16, 3)
-        matmul(17, 0)
-        add_prior(12)
-        gather_y(1)
-        turn_y(2)
-        scale_product(14)
+        store_y(2, 4, 0, 2)
+        matmul(15, 2)
+        gather_y(4, 2)
+        matmul(15, 3)
+        quantize_e(2, 3)
+        matmul(16, 0)
         round_y(6, "s")
-        matmul(17, 1)
-        matmul(17, 2)
-        quantize_y(1)
-        gather_y(2)
-        matmul(17, 3)
-        add_prior(13)
-        matmul(18, 0)
+        matmul(16, 1)
+        add_prior(12)
+        matmul(16, 2)
         round_y(7, "s")
-        matmul(18, 1)
-        quantize_y(2)
-        store_y(6)
-        matmul(18, 2)
-        scale_product(15)
+        matmul(16, 3)
+        scale_product(14)
+        matmul(17, 0)
         round_y(8, "s")
-        turn_y(3)
-        add_prior(14)
+        turn_y(6, 2)
+        add_prior(13)
         round_y(9, "s")
-        matmul(18, 3)
-        matmul(19, 0)
-        scale_product(16)
-        gather_y(3)
-        turn_y(4)
-        add_prior(15)
+        matmul(17, 1)
+        scale_product(15)
+        store_y(4, 6, 1, 2)
+        matmul(17, 2)
+        gather_y(6, 2)
+        turn_y(8, 2)
+        add_prior(14)
         round_y(10, "s")
-        matmul(19, 1)
-        quantize_y(3)
-        matmul(19, 2)
-        gather_y(4)
-        store_y(7)
-        matmul(19, 3)
-        scale_product(17)
-        store_words(0, 0, 4)
-        store_scales(0, 0)
-        matmul(20, 0)
+        scale_product(16)
+        matmul(17, 3)
+        matmul(18, 0)
+        gather_y(8, 2)
+        add_prior(15)
+        matmul(18, 1)
+        matmul(18, 2)
         round_y(11, "s")
-        store_scales(0, 1)
-        store_scales(0, 2)
-        matmul(20, 1)
-        quantize_y(4)
-        store_scales(0, 3)
-        matmul(20, 2)
-        add_prior(16)
+        scale_product(17)
+        matmul(18, 3)
+        store_y(6, 8, 1, 2)
+        matmul(19, 0)
         round_y(12, "s")
-        turn_y(5)
-        scale_product(18)
+        round_y(15, "v")
+        turn_y(10, 2)
+        add_prior(16)
         round_y(13, "s")
-        matmul(20, 3)
-        matmul(21, 0)
-        add_prior(17)
-        gather_y(5)
-        turn_y(6)
-        scale_product(19)
+        matmul(19, 1)
+        scale_product(18)
+        matmul(19, 2)
         round_y(14, "s")
-        store_y(8)
-        matmul(21, 1)
-        quantize_y(5)
-        matmul(21, 2)
-        gather_y(6)
-        matmul(21, 3)
-        add_prior(18)
-        matmul(22, 0)
-        round_y(15, "s")
-        quantize_y(6)
-        matmul(22, 1)
-        matmul(22, 2)
-        scale_product(20)
+        turn_y(12, 2)
+        add_prior(17)
         round_y(16, "s")
-        turn_y(7)
-        add_prior(19)
+        matmul(19, 3)
+        quantize_y(4, 2)
+        matmul(20, 0)
         round_y(17, "s")
-        matmul(22, 3)
-        scale_product(21)
-        matmul(23, 0)
-        gather_y(7)
-        store_y(9)
-        turn_y(8)
-        add_prior(20)
+        store_y(0, 2, 2, 3)
+        quantize_y(6, 2)
+        matmul(20, 1)
+        matmul(20, 2)
+        scale_product(19)
+        gather_y(10, 2)
+        matmul(20, 3)
+        store_words(0, 0, 8)
+        store_scales(0, 0)
+        matmul(21, 0)
+        add_prior(18)
+        store_scales(0, 1)
+        gather_y(12, 2)
+        store_scales(0, 2)
+        store_scales(0, 3)
+        turn_y(14, 2)
+        scale_product(20)
         round_y(18, "s")
-        matmul(23, 1)
-        quantize_y(7)
-        matmul(23, 2)
-        gather_y(8)
-        scale_product(22)
-        matmul(23, 3)
-        store_words(1, 0, 4)
-        store_scales(1, 0)
+        turn_y(16, 2)
+        add_prior(19)
+        matmul(21, 1)
+        quantize_y(8, 2)
+        matmul(21, 2)
         round_y(19, "s")
+        store_y(2, 4, 2, 3)
+        quantize_y(10, 2)
+        matmul(21, 3)
+        matmul(22, 0)
+        quantize_y(12, 2)
+        gather_y(14, 2)
+        matmul(22, 1)
+        scale_product(21)
+        matmul(22, 2)
+        gather_y(16, 2)
+        turn_y(18, 2)
+        add_prior(20)
+        matmul(22, 3)
+        quantize_y(14, 2)
+        matmul(23, 0)
+        gather_y(18, 2)
+        round_y(20, "v")
+        matmul(23, 1)
+        scale_product(22)
+        store_words(1, 0, 8)
+        store_scales(1, 0)
+        matmul(23, 2)
         store_scales(1, 1)
         store_scales(1, 2)
-        quantize_y(8)
+        matmul(23, 3)
         store_scales(1, 3)
         add_prior(21)
-        round_y(20, "s")
-        turn_y(9)
         scale_product(23)
         round_y(21, "s")
-        store_y(10)
+        store_y(4, 6, 2, 3)
         add_prior(22)
-        gather_y(9)
-        turn_y(10)
+        turn_y(20, 2)
         add_prior(23)
-        round_y(22, "v")
-        gather_y(10)
-        store_y(11)
+        round_y(22, "s")
+        store_y(6, 7, 2, 3)
+        quantize_y(16, 2)
+        gather_y(20, 2)
+        store_y(7, 8, 2, 3)
+        turn_y(22, 1)
         round_y(23, "v")
-        quantize_y(9)
-        turn_y(11)
-        quantize_y(10)
-        store_words(2, 0, 2)
-        store_words(2, 2, 3)
-        gather_y(11)
-        quantize_y(11)
-        store_words(2, 3, 4)
+        quantize_y(18, 2)
+        turn_y(23, 1)
+        quantize_y(20, 2)
+        gather_y(22, 1)
+        store_words(2, 0, 4)
+        quantize_y(22, 1)
+        gather_y(23, 1)
+        store_words(2, 4, 7)
+        quantize_y(23, 1)
+        store_words(2, 7, 8)
         store_scales(2, 0)
         store_scales(2, 1)
         store_scales(2, 2)

@@ -24,6 +24,16 @@ GROUPS = C // W
 ROWS = S // P
 PAIRS = ROWS // 2
 TILES = GROUPS * ROWS
+CUT = 192
+TV = 1
+KV = 2
+ADD0 = 4
+ADD1 = 0
+MIX = [3,4,5,9]
+QE = [6,11,13,14]
+TURN = [4,7,9,12,15,15,16,16,20,21,23,23,24]
+OUT = [5,9,10,15,16,16,17,20,21,22,24,24,25]
+QY = [13,14,15,18,19,20,20,22,24,24,25,26,26]
 
 
 def tile_ocean_tomography_prior_step_k2_kernel(tc, g_words, g_scales, E, D, v, a, out_0, out_1, out_2):
@@ -53,9 +63,12 @@ def tile_ocean_tomography_prior_step_k2_kernel(tc, g_words, g_scales, E, D, v, a
         e_raw, e_mix, e_code, e_scale, y_tile = {}, {}, {}, {}, {}
         g_code, d_sb, acc, step, y_sb, y_bf, turned, y_mix, y_code, y_scale, small = {}, {}, {}, {}, {}, {}, {}, {}, {}, {}, {}
 
-        def load_e(g, k):
-            e_raw[g, k] = keep.tile([P, PACK, W], BF16, name="e_raw_%d_%d" % (g, k))
-            nc.sync.dma_start(out=e_raw[g, k][:], in_=E[k * W:(k + 1) * W, g * W:(g + 1) * W].rearrange("(p t) j -> p t j", t=PACK))
+        def load_e(k, g0, g1):
+            width = g1 - g0
+            raw = work.tile([P, PACK, width * W], BF16, name="e_raw_%d" % width, tag="e_raw_%d" % width, bufs=6 if width == 1 else 2)
+            nc.sync.dma_start(out=raw[:], in_=E[k * W:(k + 1) * W, g0 * W:g1 * W].rearrange("(p t) j -> p t j", t=PACK))
+            for g in range(g0, g1):
+                e_raw[g, k] = raw[:, :, (g - g0) * W:(g - g0 + 1) * W]
 
         def load_g(m0, m1):
             codes = keep.tile([P, PASSES, (m1 - m0) * P], U32, name="g_code_%d" % m0, align_bytes=64)
@@ -64,20 +77,18 @@ def tile_ocean_tomography_prior_step_k2_kernel(tc, g_words, g_scales, E, D, v, a
                 for k in range(PASSES):
                     g_code[m, k] = codes[:, k, (m - m0) * P:(m - m0 + 1) * P]
 
-        def load_d(c, g0, g1):
-            d = keep.tile([P, 2, (g1 - g0) * W], BF16, name="d_%d_%d" % (c, g0))
-            nc.sync.dma_start(out=d[:], in_=d_view[:, 2 * c:2 * c + 2, g0 * W:g1 * W])
-            for g in range(g0, g1):
-                for h in range(2):
-                    d_sb[g * ROWS + 2 * c + h] = d[:, h, (g - g0) * W:(g - g0 + 1) * W]
+        def load_d(c):
+            d_sb[c] = keep.tile([P, 2, C], BF16, name="d_%d" % c)
+            nc.sync.dma_start(out=d_sb[c][:], in_=d_view[:, 2 * c:2 * c + 2, :])
 
         def clear():
             nc.vector.memset(ident_f32[:], 0.0)
             nc.vector.memset(g_scale[:].bitcast(U32), 0)
 
-        def load_scales(q, m0, m1):
-            nc.sync.dma_start(out=g_scale[32 * q:32 * q + 4, :, m0 * P:m1 * P].bitcast(I32),
-                              in_=g_scales[:, 4 * q:4 * q + 4, m0 * P:m1 * P].rearrange("k r n -> r k n").bitcast(I32))
+        def load_scales(m0, m1):
+            for q in range(4):
+                nc.sync.dma_start(out=g_scale[32 * q:32 * q + 4, :, m0 * P:m1 * P].bitcast(I32),
+                                  in_=g_scales[:, 4 * q:4 * q + 4, m0 * P:m1 * P].rearrange("k r n -> r k n").bitcast(I32))
 
         def prepare():
             nc.gpsimd.memset(av_rows[:], 0.0)
@@ -112,7 +123,7 @@ def tile_ocean_tomography_prior_step_k2_kernel(tc, g_words, g_scales, E, D, v, a
 
         def interleave(g, k, c0, c1, eng):
             if (g, k) not in e_mix:
-                e_mix[g, k] = work.tile([P, W, PACK], BF16, name="e_mix", tag="e_mix", bufs=4, align_bytes=64)
+                e_mix[g, k] = work.tile([P, W, PACK], BF16, name="e_mix", tag="e_mix", bufs=3, align_bytes=64)
             dst = e_mix[g, k][:, c0:c1, :].rearrange("p (c i) t -> p c t i", i=4)
             src = e_raw[g, k][:, :, c0:c1].rearrange("p t (c i) -> p c t i", i=4)
             if eng == "v":
@@ -126,377 +137,155 @@ def tile_ocean_tomography_prior_step_k2_kernel(tc, g_words, g_scales, E, D, v, a
             nc.vector.quantize_mx(out=e_code[g, k][:].bitcast(E4M3X4), scales=e_scale[g, k][:],
                                   in_=e_mix[g, k][:].rearrange("p c t -> p (c t)"))
 
-        def matmul(n, k):
-            g, m = divmod(n, ROWS)
+        def matmul(m, g, k):
             if k == 0:
-                acc[n] = acc_pool.tile([P, W], F32, name="acc", tag="acc")
-            nc.tensor.matmul_mx(out=acc[n][:], lhsT=g_code[m, k].bitcast(E5M2X4),
+                acc[m, g] = acc_pool.tile([P, W], F32, name="acc", tag="acc")
+            nc.tensor.matmul_mx(out=acc[m, g][:], lhsT=g_code[m, k].bitcast(E5M2X4),
                                 lhsT_scale=g_scale[:, k, m * P:(m + 1) * P],
                                 rhs=e_code[g, k][:].bitcast(E4M3X4), rhs_scale=e_scale[g, k][:],
                                 start=(k == 0), stop=(k == PASSES - 1))
 
-        def scale_product(n):
-            g, m = divmod(n, ROWS)
-            step[n] = work.tile([P, W], F32, name="step", tag="step", bufs=3)
-            nc.vector.scalar_tensor_tensor(out=step[n][:], in0=acc[n][:], scalar=neg_a[:, m:m + 1],
+        def scale_product(m, g):
+            if g != 1:
+                step[m, g // 2] = work.tile([P, 2 * W], F32, name="step", tag="step", bufs=4)
+            nc.vector.scalar_tensor_tensor(out=step[m, g // 2][:, (g % 2) * W:(g % 2 + 1) * W], in0=acc[m, g][:], scalar=neg_a[:, m:m + 1],
                                            in1=v_wide[:, g * W:(g + 1) * W], op0=MULT, op1=MULT)
 
-        def add_prior(n):
-            g, m = divmod(n, ROWS)
-            key = (m // 2, g // 2)
+        def add_prior(m, g0, g1):
+            key = (m // 2, g0 // 2)
             if key not in y_sb:
-                y_sb[key] = keep.tile([P, 2, (2 - g // 2) * W], F32, name="y_%d_%d" % key)
-            y_tile[n] = y_sb[key][:, m % 2, (g % 2) * W:(g % 2 + 1) * W]
-            nc.vector.scalar_tensor_tensor(out=y_tile[n], in0=d_sb[n], scalar=one_minus_a[:, m:m + 1],
-                                           in1=step[n][:], op0=MULT, op1=ADD)
+                y_sb[key] = keep.tile([P, 2, (g1 - g0) * W], F32, name="y_%d_%d" % key)
+            nc.vector.scalar_tensor_tensor(out=y_sb[key][:, m % 2, :], in0=d_sb[m // 2][:, m % 2, g0 * W:g1 * W],
+                                           scalar=one_minus_a[:, m:m + 1],
+                                           in1=step[m, g0 // 2][:, 0:(g1 - g0) * W], op0=MULT, op1=ADD)
 
-        def round_y(n, eng):
-            y_bf[n] = work.tile([P, W], BF16, name="y_bf", tag="y_bf", bufs=6)
-            dst = y_bf[n][:].rearrange("p (u c e) -> p u c e", u=2, e=2)
-            src = y_tile[n].rearrange("p (c u e) -> p u c e", u=2, e=2)
+        def round_y(m, g0, g1, eng):
+            width = (g1 - g0) * W
+            rounded = work.tile([P, width], BF16, name="y_bf", tag="y_bf", bufs=6)
+            dst = rounded[:].rearrange("p (u c e) -> p u c e", u=2, e=2)
+            src = y_sb[m // 2, g0 // 2][:, m % 2, :].rearrange("p (c u e) -> p u c e", u=2, e=2)
             if eng == "v":
                 nc.vector.tensor_copy(out=dst, in_=src)
-            elif eng == "g":
-                nc.gpsimd.tensor_scalar(out=dst, in0=src, scalar1=1.0, scalar2=0.0, op0=MULT, op1=ADD)
             else:
                 nc.scalar.copy(out=dst, in_=src)
-
-        def turn_y(n, count):
-            turned[n] = turn_pool.tile([P, count, 2, P], F32, name="turned", tag="turn")
-            for h in range(count):
-                words = y_bf[n + h][:].bitcast(F32)
+            words = rounded[:].bitcast(F32).rearrange("p (u g c) -> p u g c", u=2, c=P)
+            for g in range(g0, g1):
                 for u in range(2):
-                    nc.tensor.transpose(turned[n][:, h, u, :], words[:, u * P:(u + 1) * P], ident_f32[:])
+                    y_bf[m, g, u] = words[:, u, g - g0, :]
 
-        def gather_y(n, count):
-            y_mix[n] = work.tile([P, count * W], BF16, name="y_mix", tag="y_mix", bufs=3, align_bytes=64)
-            nc.scalar.copy(out=y_mix[n][:].bitcast(F32).rearrange("p (h i u) -> p h i u", h=count, u=2),
-                           in_=turned[n][:].rearrange("p h u i -> p h i u"))
+        def turn_y(m, count, g):
+            turned[m, g] = turn_pool.tile([P, count, 2, P], F32, name="turned", tag="turn")
+            for h in range(count):
+                for u in range(2):
+                    nc.tensor.transpose(turned[m, g][:, h, u, :], y_bf[m + h, g, u], ident_f32[:])
 
-        def quantize_y(n, count):
-            g, m = divmod(n, ROWS)
+        def gather_y(m, count, g):
+            y_mix[m, g] = work.tile([P, count * W], BF16, name="y_mix", tag="y_mix", bufs=4, align_bytes=64)
+            nc.scalar.copy(out=y_mix[m, g][:].bitcast(F32).rearrange("p (h i u) -> p h i u", h=count, u=2),
+                           in_=turned[m, g][:].rearrange("p h u i -> p h i u"))
+
+        def quantize_y(m, count, g):
             if m == 0:
                 y_code[g] = keep.tile([P, S], U32, name="y_code_%d" % g, align_bytes=64)
                 y_scale[g] = keep.tile([P, 2 * P], U8, name="y_scale_%d" % g, align_bytes=64)
             nc.vector.quantize_mx(out=y_code[g][:, m * P:(m + count) * P].bitcast(E4M3X4),
-                                  scales=y_scale[g][4 * (m // 2):P, (m % 2) * P:(m % 2 + count) * P], in_=y_mix[n][:])
+                                  scales=y_scale[g][4 * (m // 2):P, (m % 2) * P:(m % 2 + count) * P], in_=y_mix[m, g][:])
 
         def store_y(m0, m1, g0, g1):
-            nc.sync.dma_start(out=y_view[:, m0:m1, g0 * W:g1 * W], in_=y_sb[m0 // 2, g0 // 2][:, m0 % 2:m0 % 2 + m1 - m0, (g0 % 2) * W:(g0 % 2 + g1 - g0) * W])
+            nc.sync.dma_start(out=y_view[:, m0:m1, g0 * W:g1 * W], in_=y_sb[m0 // 2, g0 // 2][:, m0 % 2:m0 % 2 + m1 - m0, :])
 
         def store_words(g, m0, m1):
             nc.sync.dma_start(out=words_view[g, :, m0 * P:m1 * P], in_=y_code[g][:, m0 * P:m1 * P].bitcast(I32))
 
-        def store_scales(g, q):
-            nc.sync.dma_start(out=scales_view[g, 4 * q:4 * q + 4, :].rearrange("r (c m) -> c r m", c=PAIRS),
-                          in_=y_scale[g][32 * q:32 * q + 16, :].bitcast(I32))
+        def store_scales(g):
+            for q in range(4):
+                nc.sync.dma_start(out=scales_view[g, 4 * q:4 * q + 4, :].rearrange("r (c m) -> c r m", c=PAIRS),
+                                  in_=y_scale[g][32 * q:32 * q + 16, :].bitcast(I32))
 
         clear()
         prepare()
-        load_e(0, 0)
+        load_e(0, 0, 1)
+        load_e(0, 1, 2)
         load_av()
-        turn_av()
-        load_e(0, 1)
-        load_e(0, 2)
+        load_e(1, 0, 2)
+        load_e(2, 0, 2)
+        load_scales(0, 4)
         load_g(0, 2)
-        load_scales(0, 0, 8)
-        load_scales(1, 0, 8)
-        load_scales(2, 0, 8)
-        load_scales(3, 0, 8)
-        load_e(0, 3)
-        interleave(0, 0, 256, 512, "v")
-        interleave(0, 0, 0, 256, "s")
-        take_v()
-        spread_v(0, 1)
-        spread_v(1, 3)
+        load_e(3, 0, 1)
+        load_e(3, 1, 2)
+        load_d(0)
         load_g(2, 4)
-        interleave(0, 1, 0, 256, "v")
-        interleave(0, 1, 256, 512, "v")
-        load_e(1, 0)
-        interleave(0, 2, 0, 256, "s")
-        keep_v(0, 1)
-        interleave(0, 2, 256, 512, "v")
-        quantize_e(0, 0)
-        quantize_e(0, 1)
-        take_a()
-        load_d(0, 0, 1)
-        load_g(4, 6)
-        quantize_e(0, 2)
-        load_d(1, 0, 1)
-        load_g(6, 8)
-        load_d(2, 0, 1)
-        matmul(0, 0)
-        matmul(1, 0)
-        matmul(0, 1)
-        load_e(1, 1)
-        interleave(0, 3, 0, 192, "s")
-        keep_v(1, 3)
-        interleave(0, 3, 192, 512, "v")
-        matmul(1, 1)
-        matmul(0, 2)
-        matmul(1, 2)
-        quantize_e(0, 3)
-        load_e(1, 3)
-        matmul(0, 3)
-        matmul(1, 3)
-        matmul(2, 0)
-        scale_product(0)
-        load_e(1, 2)
-        matmul(2, 1)
-        interleave(1, 0, 0, 256, "s")
-        matmul(2, 2)
-        scale_product(1)
-        load_e(2, 0)
-        matmul(2, 3)
-        matmul(3, 0)
-        add_prior(0)
-        matmul(3, 1)
-        interleave(1, 0, 256, 512, "s")
-        matmul(3, 2)
-        scale_product(2)
-        matmul(3, 3)
-        load_d(3, 0, 1)
-        add_prior(1)
-        matmul(4, 0)
-        round_y(0, "s")
-        matmul(4, 1)
-        quantize_e(1, 0)
-        load_d(0, 1, 3)
-        matmul(4, 2)
-        round_y(1, "s")
-        matmul(4, 3)
-        scale_product(3)
-        matmul(5, 0)
-        turn_y(0, 2)
-        add_prior(2)
-        load_e(2, 1)
-        matmul(5, 1)
-        scale_product(4)
-        matmul(5, 2)
-        gather_y(0, 2)
-        matmul(5, 3)
-        load_d(1, 1, 3)
-        add_prior(3)
-        matmul(6, 0)
-        round_y(2, "s")
-        matmul(6, 1)
-        scale_product(5)
-        matmul(6, 2)
-        round_y(3, "s")
-        matmul(6, 3)
-        matmul(7, 0)
-        load_e(2, 2)
-        interleave(1, 1, 0, 256, "s")
-        interleave(1, 1, 256, 512, "v")
-        turn_y(2, 2)
-        add_prior(4)
-        matmul(7, 1)
-        matmul(7, 2)
-        gather_y(2, 2)
-        scale_product(6)
-        matmul(7, 3)
-        load_e(2, 3)
-        matmul(8, 0)
-        round_y(4, "s")
-        quantize_e(1, 1)
-        add_prior(5)
-        load_d(3, 1, 3)
-        matmul(8, 1)
-        interleave(1, 2, 0, 256, "s")
-        interleave(1, 2, 256, 512, "v")
-        interleave(1, 3, 256, 512, "v")
-        interleave(1, 3, 0, 256, "s")
-        load_d(2, 1, 3)
-        quantize_e(1, 2)
-        scale_product(7)
-        store_y(4, 6, 0, 1)
-        matmul(8, 2)
-        interleave(2, 0, 0, 256, "s")
-        quantize_e(1, 3)
-        add_prior(6)
-        matmul(8, 3)
-        interleave(2, 0, 256, 512, "s")
-        quantize_y(0, 2)
-        quantize_y(2, 2)
-        matmul(9, 0)
-        scale_product(8)
-        matmul(9, 1)
-        interleave(2, 1, 0, 256, "s")
-        matmul(9, 2)
-        quantize_e(2, 0)
-        matmul(9, 3)
-        matmul(10, 0)
-        add_prior(7)
-        matmul(10, 1)
-        interleave(2, 1, 256, 512, "s")
-        matmul(10, 2)
-        scale_product(9)
-        store_y(6, 8, 0, 1)
-        matmul(10, 3)
-        matmul(11, 0)
-        add_prior(8)
-        matmul(11, 1)
-        matmul(11, 2)
-        round_y(5, "s")
-        quantize_e(2, 1)
-        matmul(11, 3)
-        matmul(12, 0)
-        interleave(2, 2, 0, 256, "s")
-        scale_product(10)
-        turn_y(4, 2)
-        add_prior(9)
-        matmul(12, 1)
-        matmul(12, 2)
-        interleave(2, 2, 256, 512, "s")
-        scale_product(11)
-        matmul(12, 3)
-        store_y(0, 2, 0, 2)
-        matmul(13, 0)
-        add_prior(10)
-        matmul(13, 1)
-        matmul(13, 2)
-        interleave(2, 3, 0, 256, "s")
-        quantize_e(2, 2)
-        matmul(13, 3)
-        matmul(14, 0)
-        matmul(14, 1)
-        scale_product(12)
-        matmul(14, 2)
-        interleave(2, 3, 256, 512, "s")
-        matmul(14, 3)
-        add_prior(11)
-        matmul(15, 0)
-        matmul(15, 1)
-        scale_product(13)
-        store_y(2, 4, 0, 2)
-        matmul(15, 2)
-        gather_y(4, 2)
-        matmul(15, 3)
-        quantize_e(2, 3)
-        matmul(16, 0)
-        round_y(6, "s")
-        matmul(16, 1)
-        add_prior(12)
-        matmul(16, 2)
-        round_y(7, "s")
-        matmul(16, 3)
-        scale_product(14)
-        matmul(17, 0)
-        round_y(8, "s")
-        turn_y(6, 2)
-        add_prior(13)
-        round_y(9, "s")
-        matmul(17, 1)
-        scale_product(15)
-        store_y(4, 6, 1, 2)
-        matmul(17, 2)
-        gather_y(6, 2)
-        turn_y(8, 2)
-        add_prior(14)
-        round_y(10, "s")
-        scale_product(16)
-        matmul(17, 3)
-        matmul(18, 0)
-        gather_y(8, 2)
-        add_prior(15)
-        matmul(18, 1)
-        matmul(18, 2)
-        round_y(11, "s")
-        scale_product(17)
-        matmul(18, 3)
-        store_y(6, 8, 1, 2)
-        matmul(19, 0)
-        round_y(12, "s")
-        round_y(15, "v")
-        turn_y(10, 2)
-        add_prior(16)
-        round_y(13, "s")
-        matmul(19, 1)
-        scale_product(18)
-        matmul(19, 2)
-        round_y(14, "s")
-        turn_y(12, 2)
-        add_prior(17)
-        round_y(16, "s")
-        matmul(19, 3)
-        quantize_y(4, 2)
-        matmul(20, 0)
-        round_y(17, "s")
-        store_y(0, 2, 2, 3)
-        quantize_y(6, 2)
-        matmul(20, 1)
-        matmul(20, 2)
-        scale_product(19)
-        gather_y(10, 2)
-        matmul(20, 3)
-        store_words(0, 0, 8)
-        store_scales(0, 0)
-        matmul(21, 0)
-        add_prior(18)
-        store_scales(0, 1)
-        gather_y(12, 2)
-        store_scales(0, 2)
-        store_scales(0, 3)
-        turn_y(14, 2)
-        scale_product(20)
-        round_y(18, "s")
-        turn_y(16, 2)
-        add_prior(19)
-        matmul(21, 1)
-        quantize_y(8, 2)
-        matmul(21, 2)
-        round_y(19, "s")
-        store_y(2, 4, 2, 3)
-        quantize_y(10, 2)
-        matmul(21, 3)
-        matmul(22, 0)
-        quantize_y(12, 2)
-        gather_y(14, 2)
-        matmul(22, 1)
-        scale_product(21)
-        matmul(22, 2)
-        gather_y(16, 2)
-        turn_y(18, 2)
-        add_prior(20)
-        matmul(22, 3)
-        quantize_y(14, 2)
-        matmul(23, 0)
-        gather_y(18, 2)
-        round_y(20, "v")
-        matmul(23, 1)
-        scale_product(22)
-        store_words(1, 0, 8)
-        store_scales(1, 0)
-        matmul(23, 2)
-        store_scales(1, 1)
-        store_scales(1, 2)
-        matmul(23, 3)
-        store_scales(1, 3)
-        add_prior(21)
-        scale_product(23)
-        round_y(21, "s")
-        store_y(4, 6, 2, 3)
-        add_prior(22)
-        turn_y(20, 2)
-        add_prior(23)
-        round_y(22, "s")
-        store_y(6, 7, 2, 3)
-        quantize_y(16, 2)
-        gather_y(20, 2)
-        store_y(7, 8, 2, 3)
-        turn_y(22, 1)
-        round_y(23, "v")
-        quantize_y(18, 2)
-        turn_y(23, 1)
-        quantize_y(20, 2)
-        gather_y(22, 1)
-        store_words(2, 0, 4)
-        quantize_y(22, 1)
-        gather_y(23, 1)
-        store_words(2, 4, 7)
-        quantize_y(23, 1)
-        store_words(2, 7, 8)
-        store_scales(2, 0)
-        store_scales(2, 1)
-        store_scales(2, 2)
-        store_scales(2, 3)
+        load_e(0, 2, 3)
+        load_scales(4, ROWS)
+        load_g(4, ROWS)
+        load_e(1, 2, 3)
+        load_d(1)
+        load_e(2, 2, 3)
+        load_e(3, 2, 3)
+        load_d(2)
+        load_d(3)
+
+        tiles = [(2 * c + h, g) for c in range(PAIRS) for g in range(2) for h in range(2)] + [(m, 2) for m in range(ROWS)]
+
+        turn_av()
+        pieces = [(g, k) for k in range(PASSES) for g in range(2)]
+        for j, (g, k) in enumerate(pieces):
+            cut = CUT if k == PASSES - 1 else W // 2
+            interleave(g, k, 0, cut, "s")
+            interleave(g, k, cut, W, "v")
+            if j >= 1:
+                quantize_e(*pieces[j - 1])
+            if j == TV:
+                take_v()
+                take_a()
+                spread_v(0, 2)
+                spread_v(2, 3)
+            if j == KV:
+                keep_v(0, 2)
+        quantize_e(*pieces[-1])
+        for k in range(PASSES):
+            for n in range(4):
+                matmul(tiles[n][0], tiles[n][1], k)
+        keep_v(2, 3)
+
+        units = [(2 * c, 2, g) for c in range(PAIRS) for g in range(2)] + [(2 * c, 2, 2) for c in range(PAIRS - 1)] + [(ROWS - 2, 1, 2), (ROWS - 1, 1, 2)]
+        issued = 4
+        for n in range(-1, TILES + 3):
+            if 0 <= n < TILES:
+                scale_product(*tiles[n])
+            for m in range(ROWS):
+                if n == 4 * (m // 2) + ADD0 + (m % 2) * ADD1:
+                    add_prior(m, 0, 2)
+                    round_y(m, 0, 2, "s")
+                    if m % 2 == 1:
+                        store_y(m - 1, m + 1, 0, 2)
+                if n == 2 * ROWS + m + 1:
+                    add_prior(m, 2, 3)
+                    round_y(m, 2, 3, "v" if m == ROWS - 1 else "s")
+                    if m >= ROWS - 2:
+                        store_y(m, m + 1, 2, 3)
+                    elif m % 2 == 1:
+                        store_y(m - 1, m + 1, 2, 3)
+            if n in QE:
+                quantize_e(2, QE.index(n))
+            for u, unit in enumerate(units):
+                if n == QY[u]:
+                    quantize_y(*unit)
+                    m, count, g = unit
+                    bounds = (0, 4, ROWS) if g < 2 else (0, 4, 6, ROWS)
+                    if m + count in bounds:
+                        store_words(g, bounds[bounds.index(m + count) - 1], m + count)
+                    if m + count == ROWS:
+                        store_scales(g)
+            for u, unit in enumerate(units):
+                if n == OUT[u]:
+                    gather_y(*unit)
+            for u, unit in enumerate(units):
+                if n == TURN[u]:
+                    turn_y(*unit)
+            if n in MIX:
+                interleave(2, MIX.index(n), 0, W, "s")
+            while issued < min(TILES, n + 7) and (issued < 2 * ROWS or n >= QE[-1]):
+                for k in range(PASSES):
+                    matmul(tiles[issued][0], tiles[issued][1], k)
+                issued += 1

@@ -18,22 +18,30 @@ ADD = mybir.AluOpType.add
 
 P = 128
 PACK = 4
-W = 512
+QUADS = 4
+W = P * PACK
 PASSES = R // W
-GROUPS = C // W
 ROWS = S // P
-PAIRS = ROWS // 2
-TILES = GROUPS * ROWS
-CUT = 192
-TV = 1
-KV = 2
-ADD0 = 4
-ADD1 = 0
-MIX = [3,4,5,9]
-QE = [6,11,13,14]
-TURN = [4,7,9,12,15,15,16,16,20,21,23,23,24]
-OUT = [5,9,10,15,16,16,17,20,21,22,24,24,25]
-QY = [13,14,15,18,19,20,20,22,24,24,25,26,26]
+V_ROWS = C // P
+LAST_GROUP = C // W - 1
+ACC_BANKS = 6
+
+TILES = [(m + h, g) for m in range(0, ROWS, 2) for g in range(2) for h in range(2)] + [(m, LAST_GROUP) for m in range(ROWS)]
+FIRST_LATE_STEP = 2 * ROWS
+
+UNITS = ([(m, 2, g) for m in range(0, ROWS, 2) for g in range(2)]
+         + [(m, 2, LAST_GROUP) for m in range(0, ROWS - 2, 2)]
+         + [(ROWS - 2, 1, LAST_GROUP), (ROWS - 1, 1, LAST_GROUP)])
+
+SCALAR_COLUMNS_LAST = 288
+
+MIX_STEP = [-1, 2, 4, 9]
+QUANT_E_STEP = [5, 9, 10, 14]
+TURN_STEP = [4, 5, 10, 10, 15, 15, 16, 17, 19, 20, 22, 23, 24]
+GATHER_STEP = [5, 10, 11, 11, 16, 16, 17, 20, 21, 22, 24, 25, 25]
+QUANT_Y_STEP = [10, 14, 14, 15, 19, 19, 20, 22, 25, 26, 26, 26, 26]
+
+WORD_CUTS = {0: (0, 4, ROWS), 1: (0, 4, ROWS), 2: (0, 4, 6, ROWS)}
 
 
 def tile_ocean_tomography_prior_step_k2_kernel(tc, g_words, g_scales, E, D, v, a, out_0, out_1, out_2):
@@ -41,15 +49,15 @@ def tile_ocean_tomography_prior_step_k2_kernel(tc, g_words, g_scales, E, D, v, a
     with ExitStack() as ctx:
         keep = ctx.enter_context(tc.tile_pool(name="keep", bufs=1))
         work = ctx.enter_context(tc.tile_pool(name="work", bufs=3))
-        acc_pool = ctx.enter_context(tc.psum_pool(name="acc", bufs=6))
-        turn_pool = ctx.enter_context(tc.psum_pool(name="turn", bufs=2))
+        acc_pool = ctx.enter_context(tc.psum_pool(name="acc", bufs=ACC_BANKS))
+        turn_pool = ctx.enter_context(tc.psum_pool(name="turn", bufs=8 - ACC_BANKS))
         ctx.enter_context(tc.manual_schedule())
 
         g_scale = keep.tile([P, PASSES, S], U8, align_bytes=64)
         ident_f32 = keep.tile([P, P], F32)
         ident_bf16 = keep.tile([P, P], BF16)
         av_rows = keep.tile([P, P], BF16)
-        v_cols = keep.tile([P, C // P], BF16)
+        v_cols = keep.tile([P, V_ROWS], BF16)
         v_wide = keep.tile([P, C], BF16)
         neg_a = keep.tile([P, ROWS], F32)
         one_minus_a = keep.tile([P, ROWS], F32)
@@ -57,15 +65,16 @@ def tile_ocean_tomography_prior_step_k2_kernel(tc, g_words, g_scales, E, D, v, a
         g_view = g_words.rearrange("k p n t -> p k (n t)").bitcast(I32)
         d_view = D.rearrange("(m p) j -> p m j", p=P)
         y_view = out_0.rearrange("(m p) j -> p m j", p=P)
-        words_view = out_1.rearrange("g p m t -> g p (m t)").bitcast(I32)
+        words_view = out_1.rearrange("g p n t -> g p (n t)").bitcast(I32)
         scales_view = out_2.bitcast(I32)
 
-        e_raw, e_mix, e_code, e_scale, y_tile = {}, {}, {}, {}, {}
-        g_code, d_sb, acc, step, y_sb, y_bf, turned, y_mix, y_code, y_scale, small = {}, {}, {}, {}, {}, {}, {}, {}, {}, {}, {}
+        e_raw, e_mix, e_code, e_scale, g_code, d_pair = {}, {}, {}, {}, {}, {}
+        acc, scaled, y_pair, y_words, turned, y_mix, y_code, y_scale, v_psum = {}, {}, {}, {}, {}, {}, {}, {}, {}
 
         def load_e(k, g0, g1):
-            width = g1 - g0
-            raw = work.tile([P, PACK, width * W], BF16, name="e_raw_%d" % width, tag="e_raw_%d" % width, bufs=6 if width == 1 else 2)
+            groups = g1 - g0
+            raw = work.tile([P, PACK, groups * W], BF16, name="e_raw_%d" % groups, tag="e_raw_%d" % groups,
+                            bufs=6 if groups == 1 else 2)
             nc.sync.dma_start(out=raw[:], in_=E[k * W:(k + 1) * W, g0 * W:g1 * W].rearrange("(p t) j -> p t j", t=PACK))
             for g in range(g0, g1):
                 e_raw[g, k] = raw[:, :, (g - g0) * W:(g - g0 + 1) * W]
@@ -77,59 +86,35 @@ def tile_ocean_tomography_prior_step_k2_kernel(tc, g_words, g_scales, E, D, v, a
                 for k in range(PASSES):
                     g_code[m, k] = codes[:, k, (m - m0) * P:(m - m0 + 1) * P]
 
-        def load_d(c):
-            d_sb[c] = keep.tile([P, 2, C], BF16, name="d_%d" % c)
-            nc.sync.dma_start(out=d_sb[c][:], in_=d_view[:, 2 * c:2 * c + 2, :])
-
-        def clear():
-            nc.vector.memset(ident_f32[:], 0.0)
-            nc.vector.memset(g_scale[:].bitcast(U32), 0)
-
-        def load_scales(m0, m1):
-            for q in range(4):
+        def load_g_scales(m0, m1):
+            for q in range(QUADS):
                 nc.sync.dma_start(out=g_scale[32 * q:32 * q + 4, :, m0 * P:m1 * P].bitcast(I32),
                                   in_=g_scales[:, 4 * q:4 * q + 4, m0 * P:m1 * P].rearrange("k r n -> r k n").bitcast(I32))
 
-        def prepare():
-            nc.gpsimd.memset(av_rows[:], 0.0)
-            make_identity(nc, ident_f32[:], nomemset=True)
-            nc.vector.tensor_copy(out=ident_bf16[:], in_=ident_f32[:])
+        def load_d(pair):
+            d_pair[pair] = keep.tile([P, 2, C], BF16, name="d_%d" % pair)
+            nc.sync.dma_start(out=d_pair[pair][:], in_=d_view[:, 2 * pair:2 * pair + 2, :])
 
         def load_av():
             v_rows = v.rearrange("(c p) -> c p", p=P)
             nc.sync.dma_start(out=av_rows[0:ROWS, :], in_=a.rearrange("(m p) -> m p", p=P))
-            nc.sync.dma_start(out=av_rows[ROWS:2 * ROWS, :], in_=v_rows[0:ROWS, :])
-            nc.sync.dma_start(out=av_rows[2 * ROWS:ROWS + C // P, :], in_=v_rows[ROWS:C // P, :])
-
-        def turn_av():
-            small["av"] = acc_pool.tile([P, P], BF16, name="av_cols", tag="acc")
-            nc.tensor.transpose(small["av"][:], av_rows[:], ident_bf16[:])
-
-        def take_v():
-            nc.scalar.copy(out=v_cols[:], in_=small["av"][:, ROWS:ROWS + C // P])
-
-        def take_a():
-            nc.vector.tensor_scalar(out=neg_a[:], in0=small["av"][:, 0:ROWS], scalar1=-1.0, scalar2=None, op0=MULT)
-            nc.vector.tensor_scalar(out=one_minus_a[:], in0=small["av"][:, 0:ROWS], scalar1=-1.0, scalar2=1.0, op0=MULT, op1=ADD)
+            nc.sync.dma_start(out=av_rows[ROWS:ROWS + 8, :], in_=v_rows[0:8, :])
+            nc.sync.dma_start(out=av_rows[ROWS + 8:ROWS + V_ROWS, :], in_=v_rows[8:V_ROWS, :])
 
         def spread_v(g0, g1):
-            small["v", g0] = turn_pool.tile([P, (g1 - g0) * W], BF16, name="v_psum", tag="turn")
-            for c in range(g0 * PACK, g1 * PACK):
-                cc = c - g0 * PACK
-                nc.tensor.transpose(small["v", g0][:, cc * P:(cc + 1) * P], v_cols[:, c:c + 1].to_broadcast([P, P]), ident_bf16[:])
+            v_psum[g0] = turn_pool.tile([P, (g1 - g0) * W], BF16, name="v_psum", tag="turn")
+            for c in range((g1 - g0) * PACK):
+                column = v_cols[:, g0 * PACK + c:g0 * PACK + c + 1]
+                nc.tensor.transpose(v_psum[g0][:, c * P:(c + 1) * P], column.to_broadcast([P, P]), ident_bf16[:])
 
         def keep_v(g0, g1):
-            nc.scalar.copy(out=v_wide[:, g0 * W:g1 * W], in_=small["v", g0][:])
+            nc.scalar.copy(out=v_wide[:, g0 * W:g1 * W], in_=v_psum[g0][:])
 
-        def interleave(g, k, c0, c1, eng):
+        def interleave(g, k, c0, c1, copy):
             if (g, k) not in e_mix:
                 e_mix[g, k] = work.tile([P, W, PACK], BF16, name="e_mix", tag="e_mix", bufs=3, align_bytes=64)
-            dst = e_mix[g, k][:, c0:c1, :].rearrange("p (c i) t -> p c t i", i=4)
-            src = e_raw[g, k][:, :, c0:c1].rearrange("p t (c i) -> p c t i", i=4)
-            if eng == "v":
-                nc.vector.tensor_copy(out=dst, in_=src)
-            else:
-                nc.scalar.copy(out=dst, in_=src)
+            copy(out=e_mix[g, k][:, c0:c1, :].rearrange("p (c i) t -> p c t i", i=4),
+                 in_=e_raw[g, k][:, :, c0:c1].rearrange("p t (c i) -> p c t i", i=4))
 
         def quantize_e(g, k):
             e_code[g, k] = keep.tile([P, W], U32, name="e_code_%d_%d" % (g, k), align_bytes=64)
@@ -147,37 +132,32 @@ def tile_ocean_tomography_prior_step_k2_kernel(tc, g_words, g_scales, E, D, v, a
 
         def scale_product(m, g):
             if g != 1:
-                step[m, g // 2] = work.tile([P, 2 * W], F32, name="step", tag="step", bufs=4)
-            nc.vector.scalar_tensor_tensor(out=step[m, g // 2][:, (g % 2) * W:(g % 2 + 1) * W], in0=acc[m, g][:], scalar=neg_a[:, m:m + 1],
-                                           in1=v_wide[:, g * W:(g + 1) * W], op0=MULT, op1=MULT)
+                scaled[m, g // 2] = work.tile([P, 2 * W], F32, name="scaled", tag="scaled", bufs=4)
+            nc.vector.scalar_tensor_tensor(out=scaled[m, g // 2][:, (g % 2) * W:(g % 2 + 1) * W], in0=acc[m, g][:],
+                                           scalar=neg_a[:, m:m + 1], in1=v_wide[:, g * W:(g + 1) * W], op0=MULT, op1=MULT)
 
         def add_prior(m, g0, g1):
             key = (m // 2, g0 // 2)
-            if key not in y_sb:
-                y_sb[key] = keep.tile([P, 2, (g1 - g0) * W], F32, name="y_%d_%d" % key)
-            nc.vector.scalar_tensor_tensor(out=y_sb[key][:, m % 2, :], in0=d_sb[m // 2][:, m % 2, g0 * W:g1 * W],
+            if key not in y_pair:
+                y_pair[key] = keep.tile([P, 2, (g1 - g0) * W], F32, name="y_%d_%d" % key)
+            nc.vector.scalar_tensor_tensor(out=y_pair[key][:, m % 2, :], in0=d_pair[m // 2][:, m % 2, g0 * W:g1 * W],
                                            scalar=one_minus_a[:, m:m + 1],
-                                           in1=step[m, g0 // 2][:, 0:(g1 - g0) * W], op0=MULT, op1=ADD)
+                                           in1=scaled[m, g0 // 2][:, 0:(g1 - g0) * W], op0=MULT, op1=ADD)
 
-        def round_y(m, g0, g1, eng):
-            width = (g1 - g0) * W
-            rounded = work.tile([P, width], BF16, name="y_bf", tag="y_bf", bufs=6)
-            dst = rounded[:].rearrange("p (u c e) -> p u c e", u=2, e=2)
-            src = y_sb[m // 2, g0 // 2][:, m % 2, :].rearrange("p (c u e) -> p u c e", u=2, e=2)
-            if eng == "v":
-                nc.vector.tensor_copy(out=dst, in_=src)
-            else:
-                nc.scalar.copy(out=dst, in_=src)
+        def round_y(m, g0, g1, copy):
+            rounded = work.tile([P, (g1 - g0) * W], BF16, name="rounded", tag="rounded", bufs=6)
+            copy(out=rounded[:].rearrange("p (u c e) -> p u c e", u=2, e=2),
+                 in_=y_pair[m // 2, g0 // 2][:, m % 2, :].rearrange("p (c u e) -> p u c e", u=2, e=2))
             words = rounded[:].bitcast(F32).rearrange("p (u g c) -> p u g c", u=2, c=P)
             for g in range(g0, g1):
                 for u in range(2):
-                    y_bf[m, g, u] = words[:, u, g - g0, :]
+                    y_words[m, g, u] = words[:, u, g - g0, :]
 
         def turn_y(m, count, g):
             turned[m, g] = turn_pool.tile([P, count, 2, P], F32, name="turned", tag="turn")
             for h in range(count):
                 for u in range(2):
-                    nc.tensor.transpose(turned[m, g][:, h, u, :], y_bf[m + h, g, u], ident_f32[:])
+                    nc.tensor.transpose(turned[m, g][:, h, u, :], y_words[m + h, g, u], ident_f32[:])
 
         def gather_y(m, count, g):
             y_mix[m, g] = work.tile([P, count * W], BF16, name="y_mix", tag="y_mix", bufs=4, align_bytes=64)
@@ -192,100 +172,104 @@ def tile_ocean_tomography_prior_step_k2_kernel(tc, g_words, g_scales, E, D, v, a
                                   scales=y_scale[g][4 * (m // 2):P, (m % 2) * P:(m % 2 + count) * P], in_=y_mix[m, g][:])
 
         def store_y(m0, m1, g0, g1):
-            nc.sync.dma_start(out=y_view[:, m0:m1, g0 * W:g1 * W], in_=y_sb[m0 // 2, g0 // 2][:, m0 % 2:m0 % 2 + m1 - m0, :])
+            nc.sync.dma_start(out=y_view[:, m0:m1, g0 * W:g1 * W],
+                              in_=y_pair[m0 // 2, g0 // 2][:, m0 % 2:m0 % 2 + m1 - m0, :])
 
         def store_words(g, m0, m1):
             nc.sync.dma_start(out=words_view[g, :, m0 * P:m1 * P], in_=y_code[g][:, m0 * P:m1 * P].bitcast(I32))
 
         def store_scales(g):
-            for q in range(4):
-                nc.sync.dma_start(out=scales_view[g, 4 * q:4 * q + 4, :].rearrange("r (c m) -> c r m", c=PAIRS),
+            for q in range(QUADS):
+                nc.sync.dma_start(out=scales_view[g, 4 * q:4 * q + 4, :].rearrange("r (j n) -> j r n", j=ROWS // 2),
                                   in_=y_scale[g][32 * q:32 * q + 16, :].bitcast(I32))
 
-        clear()
-        prepare()
+        nc.vector.memset(ident_f32[:], 0.0)
+        nc.vector.memset(g_scale[:].bitcast(U32), 0)
+        nc.gpsimd.memset(av_rows[:], 0.0)
+        make_identity(nc, ident_f32[:], nomemset=True)
+        nc.vector.tensor_copy(out=ident_bf16[:], in_=ident_f32[:])
+
         load_e(0, 0, 1)
         load_e(0, 1, 2)
         load_av()
         load_e(1, 0, 2)
+        load_g_scales(0, 4)
         load_e(2, 0, 2)
-        load_scales(0, 4)
         load_g(0, 2)
         load_e(3, 0, 1)
         load_e(3, 1, 2)
-        load_d(0)
-        load_g(2, 4)
         load_e(0, 2, 3)
-        load_scales(4, ROWS)
-        load_g(4, ROWS)
+        load_g(2, 4)
+        load_d(0)
         load_e(1, 2, 3)
+        load_g_scales(4, ROWS)
+        load_g(4, 6)
         load_d(1)
         load_e(2, 2, 3)
+        load_g(6, ROWS)
         load_e(3, 2, 3)
         load_d(2)
         load_d(3)
 
-        tiles = [(2 * c + h, g) for c in range(PAIRS) for g in range(2) for h in range(2)] + [(m, 2) for m in range(ROWS)]
-
-        turn_av()
+        av_cols = acc_pool.tile([P, P], BF16, name="av_cols", tag="acc")
+        nc.tensor.transpose(av_cols[:], av_rows[:], ident_bf16[:])
         pieces = [(g, k) for k in range(PASSES) for g in range(2)]
         for j, (g, k) in enumerate(pieces):
-            cut = CUT if k == PASSES - 1 else W // 2
-            interleave(g, k, 0, cut, "s")
-            interleave(g, k, cut, W, "v")
+            cut = SCALAR_COLUMNS_LAST if k == PASSES - 1 else W // 2
+            interleave(g, k, 0, cut, nc.scalar.copy)
+            interleave(g, k, cut, W, nc.vector.tensor_copy)
             if j >= 1:
                 quantize_e(*pieces[j - 1])
-            if j == TV:
-                take_v()
-                take_a()
+            if j == 1:
+                nc.scalar.copy(out=v_cols[:], in_=av_cols[:, ROWS:ROWS + V_ROWS])
+                nc.vector.tensor_scalar(out=neg_a[:], in0=av_cols[:, 0:ROWS], scalar1=-1.0, scalar2=None, op0=MULT)
+                nc.vector.tensor_scalar(out=one_minus_a[:], in0=av_cols[:, 0:ROWS], scalar1=-1.0, scalar2=1.0, op0=MULT, op1=ADD)
                 spread_v(0, 2)
                 spread_v(2, 3)
-            if j == KV:
+            if j == 2:
                 keep_v(0, 2)
         quantize_e(*pieces[-1])
-        for k in range(PASSES):
-            for n in range(4):
-                matmul(tiles[n][0], tiles[n][1], k)
+        for g, k in pieces:
+            matmul(0, g, k)
+            matmul(1, g, k)
         keep_v(2, 3)
 
-        units = [(2 * c, 2, g) for c in range(PAIRS) for g in range(2)] + [(2 * c, 2, 2) for c in range(PAIRS - 1)] + [(ROWS - 2, 1, 2), (ROWS - 1, 1, 2)]
         issued = 4
-        for n in range(-1, TILES + 3):
-            if 0 <= n < TILES:
-                scale_product(*tiles[n])
+        for step in range(-1, QUANT_Y_STEP[-1] + 1):
+            if 0 <= step < len(TILES):
+                scale_product(*TILES[step])
             for m in range(ROWS):
-                if n == 4 * (m // 2) + ADD0 + (m % 2) * ADD1:
+                if step == 4 * (m // 2 + 1):
                     add_prior(m, 0, 2)
-                    round_y(m, 0, 2, "s")
+                    round_y(m, 0, 2, nc.scalar.copy)
                     if m % 2 == 1:
                         store_y(m - 1, m + 1, 0, 2)
-                if n == 2 * ROWS + m + 1:
+                if step == FIRST_LATE_STEP + m + 1:
                     add_prior(m, 2, 3)
-                    round_y(m, 2, 3, "v" if m == ROWS - 1 else "s")
+                    round_y(m, 2, 3, nc.vector.tensor_copy if m == ROWS - 1 else nc.scalar.copy)
                     if m >= ROWS - 2:
                         store_y(m, m + 1, 2, 3)
                     elif m % 2 == 1:
                         store_y(m - 1, m + 1, 2, 3)
-            if n in QE:
-                quantize_e(2, QE.index(n))
-            for u, unit in enumerate(units):
-                if n == QY[u]:
-                    quantize_y(*unit)
-                    m, count, g = unit
-                    bounds = (0, 4, ROWS) if g < 2 else (0, 4, 6, ROWS)
-                    if m + count in bounds:
-                        store_words(g, bounds[bounds.index(m + count) - 1], m + count)
+            if step in QUANT_E_STEP:
+                quantize_e(LAST_GROUP, QUANT_E_STEP.index(step))
+            for u, (m, count, g) in enumerate(UNITS):
+                if step == QUANT_Y_STEP[u]:
+                    quantize_y(m, count, g)
+                    cuts = WORD_CUTS[g]
+                    if m + count in cuts:
+                        store_words(g, cuts[cuts.index(m + count) - 1], m + count)
                     if m + count == ROWS:
                         store_scales(g)
-            for u, unit in enumerate(units):
-                if n == OUT[u]:
+            for u, unit in enumerate(UNITS):
+                if step == GATHER_STEP[u]:
                     gather_y(*unit)
-            for u, unit in enumerate(units):
-                if n == TURN[u]:
+            for u, unit in enumerate(UNITS):
+                if step == TURN_STEP[u]:
                     turn_y(*unit)
-            if n in MIX:
-                interleave(2, MIX.index(n), 0, W, "s")
-            while issued < min(TILES, n + 7) and (issued < 2 * ROWS or n >= QE[-1]):
+            if step in MIX_STEP:
+                interleave(LAST_GROUP, MIX_STEP.index(step), 0, W, nc.scalar.copy)
+            while issued < min(len(TILES), step + 1 + ACC_BANKS) and (issued < FIRST_LATE_STEP or step >= QUANT_E_STEP[-1]):
                 for k in range(PASSES):
-                    matmul(tiles[issued][0], tiles[issued][1], k)
+                    matmul(*TILES[issued], k)
                 issued += 1

from contextlib import ExitStack

import concourse.mybir as mybir
from concourse.masks import make_identity

R, S, C = 2048, 1024, 1536
FLOPS = 2 * R * S * C

F32 = mybir.dt.float32
BF16 = mybir.dt.bfloat16
I32 = mybir.dt.int32
U32 = mybir.dt.uint32
U8 = mybir.dt.uint8
E4M3X4 = mybir.dt.float8_e4m3fn_x4
E5M2X4 = mybir.dt.float8_e5m2_x4
MULT = mybir.AluOpType.mult
ADD = mybir.AluOpType.add

P = 128
PACK = 4
QUADS = 4
W = P * PACK
PASSES = R // W
ROWS = S // P
V_ROWS = C // P
LAST_GROUP = C // W - 1
ACC_BANKS = 6

TILES = [(m + h, g) for m in range(0, ROWS, 2) for g in range(2) for h in range(2)] + [(m, LAST_GROUP) for m in range(ROWS)]
FIRST_LATE_STEP = 2 * ROWS

UNITS = ([(m, 2, g) for m in range(0, ROWS, 2) for g in range(2)]
         + [(m, 2, LAST_GROUP) for m in range(0, ROWS - 2, 2)]
         + [(ROWS - 2, 1, LAST_GROUP), (ROWS - 1, 1, LAST_GROUP)])

SCALAR_COLUMNS_LAST = 288

MIX_STEP = [-1, 2, 4, 9]
QUANT_E_STEP = [5, 9, 10, 14]
TURN_STEP = [4, 5, 10, 10, 15, 15, 16, 17, 19, 20, 22, 23, 24]
GATHER_STEP = [5, 10, 11, 11, 16, 16, 17, 20, 21, 22, 24, 25, 25]
QUANT_Y_STEP = [10, 14, 14, 15, 19, 19, 20, 22, 25, 26, 26, 26, 26]

WORD_CUTS = {0: (0, 4, ROWS), 1: (0, 4, ROWS), 2: (0, 4, 6, ROWS)}


def tile_ocean_tomography_prior_step_k2_kernel(tc, g_words, g_scales, E, D, v, a, out_0, out_1, out_2):
    nc = tc.nc
    with ExitStack() as ctx:
        keep = ctx.enter_context(tc.tile_pool(name="keep", bufs=1))
        work = ctx.enter_context(tc.tile_pool(name="work", bufs=3))
        acc_pool = ctx.enter_context(tc.psum_pool(name="acc", bufs=ACC_BANKS))
        turn_pool = ctx.enter_context(tc.psum_pool(name="turn", bufs=8 - ACC_BANKS))
        ctx.enter_context(tc.manual_schedule())

        g_scale = keep.tile([P, PASSES, S], U8, align_bytes=64)
        ident_f32 = keep.tile([P, P], F32)
        ident_bf16 = keep.tile([P, P], BF16)
        av_rows = keep.tile([P, P], BF16)
        v_cols = keep.tile([P, V_ROWS], BF16)
        v_wide = keep.tile([P, C], BF16)
        neg_a = keep.tile([P, ROWS], F32)
        one_minus_a = keep.tile([P, ROWS], F32)

        g_view = g_words.rearrange("k p n t -> p k (n t)").bitcast(I32)
        d_view = D.rearrange("(m p) j -> p m j", p=P)
        y_view = out_0.rearrange("(m p) j -> p m j", p=P)
        words_view = out_1.rearrange("g p n t -> g p (n t)").bitcast(I32)
        scales_view = out_2.bitcast(I32)

        e_raw, e_mix, e_code, e_scale, g_code, d_pair = {}, {}, {}, {}, {}, {}
        acc, scaled, y_pair, y_words, turned, y_mix, y_code, y_scale, v_psum = {}, {}, {}, {}, {}, {}, {}, {}, {}

        def load_e(k, g0, g1):
            groups = g1 - g0
            raw = work.tile([P, PACK, groups * W], BF16, name="e_raw_%d" % groups, tag="e_raw_%d" % groups,
                            bufs=6 if groups == 1 else 2)
            nc.sync.dma_start(out=raw[:], in_=E[k * W:(k + 1) * W, g0 * W:g1 * W].rearrange("(p t) j -> p t j", t=PACK))
            for g in range(g0, g1):
                e_raw[g, k] = raw[:, :, (g - g0) * W:(g - g0 + 1) * W]

        def load_g(m0, m1):
            codes = keep.tile([P, PASSES, (m1 - m0) * P], U32, name="g_code_%d" % m0, align_bytes=64)
            nc.sync.dma_start(out=codes[:].bitcast(I32), in_=g_view[:, :, m0 * P:m1 * P])
            for m in range(m0, m1):
                for k in range(PASSES):
                    g_code[m, k] = codes[:, k, (m - m0) * P:(m - m0 + 1) * P]

        def load_g_scales(m0, m1):
            for q in range(QUADS):
                nc.sync.dma_start(out=g_scale[32 * q:32 * q + 4, :, m0 * P:m1 * P].bitcast(I32),
                                  in_=g_scales[:, 4 * q:4 * q + 4, m0 * P:m1 * P].rearrange("k r n -> r k n").bitcast(I32))

        def load_d(pair):
            d_pair[pair] = keep.tile([P, 2, C], BF16, name="d_%d" % pair)
            nc.sync.dma_start(out=d_pair[pair][:], in_=d_view[:, 2 * pair:2 * pair + 2, :])

        def load_av():
            v_rows = v.rearrange("(c p) -> c p", p=P)
            nc.sync.dma_start(out=av_rows[0:ROWS, :], in_=a.rearrange("(m p) -> m p", p=P))
            nc.sync.dma_start(out=av_rows[ROWS:ROWS + 8, :], in_=v_rows[0:8, :])
            nc.sync.dma_start(out=av_rows[ROWS + 8:ROWS + V_ROWS, :], in_=v_rows[8:V_ROWS, :])

        def spread_v(g0, g1):
            v_psum[g0] = turn_pool.tile([P, (g1 - g0) * W], BF16, name="v_psum", tag="turn")
            for c in range((g1 - g0) * PACK):
                column = v_cols[:, g0 * PACK + c:g0 * PACK + c + 1]
                nc.tensor.transpose(v_psum[g0][:, c * P:(c + 1) * P], column.to_broadcast([P, P]), ident_bf16[:])

        def keep_v(g0, g1):
            nc.scalar.copy(out=v_wide[:, g0 * W:g1 * W], in_=v_psum[g0][:])

        def interleave(g, k, c0, c1, copy):
            if (g, k) not in e_mix:
                e_mix[g, k] = work.tile([P, W, PACK], BF16, name="e_mix", tag="e_mix", bufs=3, align_bytes=64)
            copy(out=e_mix[g, k][:, c0:c1, :].rearrange("p (c i) t -> p c t i", i=4),
                 in_=e_raw[g, k][:, :, c0:c1].rearrange("p t (c i) -> p c t i", i=4))

        def quantize_e(g, k):
            e_code[g, k] = keep.tile([P, W], U32, name="e_code_%d_%d" % (g, k), align_bytes=64)
            e_scale[g, k] = keep.tile([P, W], U8, name="e_scale_%d_%d" % (g, k), align_bytes=64)
            nc.vector.quantize_mx(out=e_code[g, k][:].bitcast(E4M3X4), scales=e_scale[g, k][:],
                                  in_=e_mix[g, k][:].rearrange("p c t -> p (c t)"))

        def matmul(m, g, k):
            if k == 0:
                acc[m, g] = acc_pool.tile([P, W], F32, name="acc", tag="acc")
            nc.tensor.matmul_mx(out=acc[m, g][:], lhsT=g_code[m, k].bitcast(E5M2X4),
                                lhsT_scale=g_scale[:, k, m * P:(m + 1) * P],
                                rhs=e_code[g, k][:].bitcast(E4M3X4), rhs_scale=e_scale[g, k][:],
                                start=(k == 0), stop=(k == PASSES - 1))

        def scale_product(m, g):
            if g != 1:
                scaled[m, g // 2] = work.tile([P, 2 * W], F32, name="scaled", tag="scaled", bufs=4)
            nc.vector.scalar_tensor_tensor(out=scaled[m, g // 2][:, (g % 2) * W:(g % 2 + 1) * W], in0=acc[m, g][:],
                                           scalar=neg_a[:, m:m + 1], in1=v_wide[:, g * W:(g + 1) * W], op0=MULT, op1=MULT)

        def add_prior(m, g0, g1):
            key = (m // 2, g0 // 2)
            if key not in y_pair:
                y_pair[key] = keep.tile([P, 2, (g1 - g0) * W], F32, name="y_%d_%d" % key)
            nc.vector.scalar_tensor_tensor(out=y_pair[key][:, m % 2, :], in0=d_pair[m // 2][:, m % 2, g0 * W:g1 * W],
                                           scalar=one_minus_a[:, m:m + 1],
                                           in1=scaled[m, g0 // 2][:, 0:(g1 - g0) * W], op0=MULT, op1=ADD)

        def round_y(m, g0, g1, copy):
            rounded = work.tile([P, (g1 - g0) * W], BF16, name="rounded", tag="rounded", bufs=6)
            copy(out=rounded[:].rearrange("p (u c e) -> p u c e", u=2, e=2),
                 in_=y_pair[m // 2, g0 // 2][:, m % 2, :].rearrange("p (c u e) -> p u c e", u=2, e=2))
            words = rounded[:].bitcast(F32).rearrange("p (u g c) -> p u g c", u=2, c=P)
            for g in range(g0, g1):
                for u in range(2):
                    y_words[m, g, u] = words[:, u, g - g0, :]

        def turn_y(m, count, g):
            turned[m, g] = turn_pool.tile([P, count, 2, P], F32, name="turned", tag="turn")
            for h in range(count):
                for u in range(2):
                    nc.tensor.transpose(turned[m, g][:, h, u, :], y_words[m + h, g, u], ident_f32[:])

        def gather_y(m, count, g):
            y_mix[m, g] = work.tile([P, count * W], BF16, name="y_mix", tag="y_mix", bufs=4, align_bytes=64)
            nc.scalar.copy(out=y_mix[m, g][:].bitcast(F32).rearrange("p (h i u) -> p h i u", h=count, u=2),
                           in_=turned[m, g][:].rearrange("p h u i -> p h i u"))

        def quantize_y(m, count, g):
            if m == 0:
                y_code[g] = keep.tile([P, S], U32, name="y_code_%d" % g, align_bytes=64)
                y_scale[g] = keep.tile([P, 2 * P], U8, name="y_scale_%d" % g, align_bytes=64)
            nc.vector.quantize_mx(out=y_code[g][:, m * P:(m + count) * P].bitcast(E4M3X4),
                                  scales=y_scale[g][4 * (m // 2):P, (m % 2) * P:(m % 2 + count) * P], in_=y_mix[m, g][:])

        def store_y(m0, m1, g0, g1):
            nc.sync.dma_start(out=y_view[:, m0:m1, g0 * W:g1 * W],
                              in_=y_pair[m0 // 2, g0 // 2][:, m0 % 2:m0 % 2 + m1 - m0, :])

        def store_words(g, m0, m1):
            nc.sync.dma_start(out=words_view[g, :, m0 * P:m1 * P], in_=y_code[g][:, m0 * P:m1 * P].bitcast(I32))

        def store_scales(g):
            for q in range(QUADS):
                nc.sync.dma_start(out=scales_view[g, 4 * q:4 * q + 4, :].rearrange("r (j n) -> j r n", j=ROWS // 2),
                                  in_=y_scale[g][32 * q:32 * q + 16, :].bitcast(I32))

        nc.vector.memset(ident_f32[:], 0.0)
        nc.vector.memset(g_scale[:].bitcast(U32), 0)
        nc.gpsimd.memset(av_rows[:], 0.0)
        make_identity(nc, ident_f32[:], nomemset=True)
        nc.vector.tensor_copy(out=ident_bf16[:], in_=ident_f32[:])

        load_e(0, 0, 1)
        load_e(0, 1, 2)
        load_av()
        load_e(1, 0, 2)
        load_g_scales(0, 4)
        load_e(2, 0, 2)
        load_g(0, 2)
        load_e(3, 0, 1)
        load_e(3, 1, 2)
        load_e(0, 2, 3)
        load_g(2, 4)
        load_d(0)
        load_e(1, 2, 3)
        load_g_scales(4, ROWS)
        load_g(4, 6)
        load_d(1)
        load_e(2, 2, 3)
        load_g(6, ROWS)
        load_e(3, 2, 3)
        load_d(2)
        load_d(3)

        av_cols = acc_pool.tile([P, P], BF16, name="av_cols", tag="acc")
        nc.tensor.transpose(av_cols[:], av_rows[:], ident_bf16[:])
        pieces = [(g, k) for k in range(PASSES) for g in range(2)]
        for j, (g, k) in enumerate(pieces):
            cut = SCALAR_COLUMNS_LAST if k == PASSES - 1 else W // 2
            interleave(g, k, 0, cut, nc.scalar.copy)
            interleave(g, k, cut, W, nc.vector.tensor_copy)
            if j >= 1:
                quantize_e(*pieces[j - 1])
            if j == 1:
                nc.scalar.copy(out=v_cols[:], in_=av_cols[:, ROWS:ROWS + V_ROWS])
                nc.vector.tensor_scalar(out=neg_a[:], in0=av_cols[:, 0:ROWS], scalar1=-1.0, scalar2=None, op0=MULT)
                nc.vector.tensor_scalar(out=one_minus_a[:], in0=av_cols[:, 0:ROWS], scalar1=-1.0, scalar2=1.0, op0=MULT, op1=ADD)
                spread_v(0, 2)
                spread_v(2, 3)
            if j == 2:
                keep_v(0, 2)
        quantize_e(*pieces[-1])
        for g, k in pieces:
            matmul(0, g, k)
            matmul(1, g, k)
        keep_v(2, 3)

        issued = 4
        for step in range(-1, QUANT_Y_STEP[-1] + 1):
            if 0 <= step < len(TILES):
                scale_product(*TILES[step])
            for m in range(ROWS):
                if step == 4 * (m // 2 + 1):
                    add_prior(m, 0, 2)
                    round_y(m, 0, 2, nc.scalar.copy)
                    if m % 2 == 1:
                        store_y(m - 1, m + 1, 0, 2)
                if step == FIRST_LATE_STEP + m + 1:
                    add_prior(m, 2, 3)
                    round_y(m, 2, 3, nc.vector.tensor_copy if m == ROWS - 1 else nc.scalar.copy)
                    if m >= ROWS - 2:
                        store_y(m, m + 1, 2, 3)
                    elif m % 2 == 1:
                        store_y(m - 1, m + 1, 2, 3)
            if step in QUANT_E_STEP:
                quantize_e(LAST_GROUP, QUANT_E_STEP.index(step))
            for u, (m, count, g) in enumerate(UNITS):
                if step == QUANT_Y_STEP[u]:
                    quantize_y(m, count, g)
                    cuts = WORD_CUTS[g]
                    if m + count in cuts:
                        store_words(g, cuts[cuts.index(m + count) - 1], m + count)
                    if m + count == ROWS:
                        store_scales(g)
            for u, unit in enumerate(UNITS):
                if step == GATHER_STEP[u]:
                    gather_y(*unit)
            for u, unit in enumerate(UNITS):
                if step == TURN_STEP[u]:
                    turn_y(*unit)
            if step in MIX_STEP:
                interleave(LAST_GROUP, MIX_STEP.index(step), 0, W, nc.scalar.copy)
            while issued < min(len(TILES), step + 1 + ACC_BANKS) and (issued < FIRST_LATE_STEP or step >= QUANT_E_STEP[-1]):
                for k in range(PASSES):
                    matmul(*TILES[issued], k)
                issued += 1
